import numpy as np
import ml_dtypes


def mxq(x, axis, fmt="e4m3"):
    dtype, down = {"e4m3": (ml_dtypes.float8_e4m3fn, 7), "e5m2": (ml_dtypes.float8_e5m2, 14)}[fmt]
    v = np.moveaxis(np.asarray(x, np.float32).astype(ml_dtypes.bfloat16).astype(np.float64), axis, -1)
    blocks = v.reshape(v.shape[:-1] + (-1, 32))
    amax = np.abs(blocks).max(-1, keepdims=True)
    byte = np.maximum(np.where(amax > 0, np.frexp(amax)[1] - 1 + 127, 0) - down, 1)
    scale = np.exp2(byte - 127.0)
    codes = (blocks / scale).astype(np.float32).astype(dtype).astype(np.float64)
    return np.moveaxis((codes * scale).reshape(v.shape), -1, axis)


WIDE = False


def mx_kscale(k):
    if not WIDE:
        return np.ones(k)
    levels = np.array([10, -10, 5, -5, 0])
    if k % 512:
        return np.exp2(np.random.permutation(np.resize(levels, k // 32))).repeat(32)
    a = np.empty((k // 512, 16))
    for p in range(k // 512):
        a[p, :8] = np.random.permutation(np.resize(levels, 8))
        for g in range(8):
            far = levels[np.abs(levels - a[p, g]) >= 10]
            a[p, g + 8] = far[np.random.randint(len(far))]
    return np.exp2(a.ravel()).repeat(32)


BF16 = ml_dtypes.bfloat16


def bf(x):
    return np.asarray(x, np.float32).astype(BF16)


def f64(x):
    return np.asarray(x).astype(np.float64)

E4M3FN = np.array([(-1.0 if i & 128 else 1.0) * ((1.0 + (i & 7) / 8.0) * 2.0 ** (((i >> 3) & 15) - 7) if i & 120 else (i & 7) * 2.0 ** -9) for i in range(256)])


def e4m3fn_bytes(y):
    return np.clip(np.asarray(y, np.float64), -448.0, 448.0).astype(np.float32).astype(ml_dtypes.float8_e4m3fn).view(np.uint8)


def e4m3fn_values(b):
    return E4M3FN[b]


P, C1, C2, R = 4096, 512, 1024, 512


def setup_inputs():
    s, t, u = mx_kscale(P), mx_kscale(C2), mx_kscale(C1)
    f = P ** 0.25 * np.random.standard_normal((P, C1)) * s[:, None]
    h = P ** 0.25 * np.random.standard_normal((P, C2)) / s[:, None]
    f_scale = (np.abs(f).max(axis=1, keepdims=True) / 448.0).astype(np.float32)
    h_scale = (np.abs(h).max(axis=1, keepdims=True) / 448.0).astype(np.float32)
    return {"F_bytes": e4m3fn_bytes(f / f64(f_scale)), "F_scale": f_scale,
            "H_bytes": e4m3fn_bytes(h / f64(h_scale)), "H_scale": h_scale,
            "A": bf(0.5 * np.random.standard_normal((C1, C2))),
            "g": bf((1 + 0.1 * np.random.standard_normal(C2)) * t),
            "e": bf((1 + 0.1 * np.random.standard_normal(C1)) * u),
            "V": bf(np.random.standard_normal((C2, R)) / np.sqrt(C2) / t[:, None]),
            "U": bf(np.random.standard_normal((R, C1)) / np.sqrt(C1) / u)}


def reference(F_bytes, F_scale, H_bytes, H_scale, A, g, e, V, U):
    F = e4m3fn_values(F_bytes) * np.repeat(f64(F_scale), C1, axis=1)
    H = e4m3fn_values(H_bytes) * np.repeat(f64(H_scale), C2, axis=1)
    G = mxq(F, 0, "e4m3").T @ mxq(H, 0, "e4m3")
    D = G / P - f64(A)
    Y = mxq(D * f64(g), 1, "e4m3") @ mxq(f64(V), 0, "e4m3")
    Z = mxq(f64(U), 1, "e4m3") @ mxq(D * f64(e)[:, None], 0, "e4m3")
    return Y, Z

@@ -1,0 +1,336 @@
+from contextlib import ExitStack
+
+import concourse.mybir as mybir
+from concourse.masks import make_identity
+
+PIXELS, C1, C2, R = 4096, 512, 1024, 512
+FLOPS = 2 * PIXELS * C1 * C2 + 2 * C1 * C2 * R + 2 * R * C1 * C2
+
+F32 = mybir.dt.float32
+BF16 = mybir.dt.bfloat16
+U32 = mybir.dt.uint32
+U8 = mybir.dt.uint8
+FP8 = mybir.dt.float8_e4m3fn
+FP8X4 = mybir.dt.float8_e4m3fn_x4
+MULT = mybir.AluOpType.mult
+SUBTRACT = mybir.AluOpType.subtract
+COPY = mybir.ActivationFunctionType.Copy
+
+P = 128
+PACK = 4
+W = 512
+PASSES = PIXELS // W
+HALVES = C2 // W
+
+CHUNKS = [(0, 512), (512, 256), (768, 256)]
+VECTOR_PLANES = {0: 2, 1: 3, 2: 4, 4: 3, 6: 4, 8: 3, 10: 3, 12: 3, 14: 3, 16: 2}
+TENSOR_UNITS = {3, 5, 7, 9, 11, 13, 15}
+
+
+def tile_cross_layer_gram_sketch_d5_kernel(tc, F_bytes, F_scale, H_bytes, H_scale, A, g, e, V, U, out_0, out_1):
+    nc = tc.nc
+    with ExitStack() as ctx:
+        keep = ctx.enter_context(tc.tile_pool(name="keep", bufs=1))
+        stage = ctx.enter_context(tc.tile_pool(name="stage", bufs=3))
+        psum = ctx.enter_context(tc.psum_pool(name="psum", bufs=1))
+        ctx.enter_context(tc.manual_schedule())
+
+        def bank(b, shape, name, dtype=F32):
+            return psum.tile(shape, dtype, name=name, tag="bank%d" % b)
+
+        f_scale = keep.tile([P, PASSES, PACK], F32, name="f_scale")
+        h_scale = keep.tile([P, PASSES, PACK], F32, name="h_scale")
+        nc.scalar.dma_start(out=f_scale[:], in_=F_scale.rearrange("(s p t) o -> p s (t o)", p=P, t=PACK))
+        nc.scalar.dma_start(out=h_scale[:], in_=H_scale.rearrange("(s p t) o -> p s (t o)", p=P, t=PACK))
+        warm_in = keep.tile([P, 1], F32, name="warm_in")
+        warm_out = keep.tile([P, 1], F32, name="warm_out")
+        nc.vector.memset(warm_in[:], 0.0)
+        nc.scalar.activation(out=warm_out[:], in_=warm_in[:], func=COPY)
+
+        ident = keep.tile([P, P], F32, name="ident")
+        make_identity(nc, ident[:])
+        ident_bf = keep.tile([P, P], BF16, name="ident_bf")
+        make_identity(nc, ident_bf[:])
+
+        F_rows = F_bytes.rearrange("(s p t) c -> s p t c", p=P, t=PACK)
+        H_rows = H_bytes.rearrange("(s p t) c -> s p t c", p=P, t=PACK)
+        f_bytes = [keep.tile([P, PACK, C1], U8, name="f_bytes%d" % s) for s in range(PASSES)]
+        h_bytes = [None] + [keep.tile([P, PACK, C2], U8, name="h_bytes%d" % s) for s in range(1, PASSES)]
+        h_first = [keep.tile([P, PACK, W], U8, name="h_bytes0_%d" % half) for half in range(HALVES)]
+        u_rows = keep.tile([P, PACK, C1], BF16, name="u_rows")
+        v_rows = keep.tile([P, HALVES, PACK, R], BF16, name="v_rows")
+        a_rows = keep.tile([P, PACK, C2], BF16, name="a_rows")
+        e_bf = keep.tile([P, PACK], BF16, name="e_bf")
+        e_col = keep.tile([P, PACK], F32, name="e_col")
+        g_spread = keep.tile([P, C2], BF16, name="g_spread")
+
+        nc.sync.dma_start(out=f_bytes[0][:, 0:2, :], in_=F_rows[0][:, 0:2, :])
+        nc.sync.dma_start(out=f_bytes[0][:, 2:4, :], in_=F_rows[0][:, 2:4, :])
+        nc.sync.dma_start(out=h_first[0][:], in_=H_rows[0][:, :, 0:W])
+        for s in range(1, PASSES):
+            nc.sync.dma_start(out=f_bytes[s][:], in_=F_rows[s])
+            nc.sync.dma_start(out=h_bytes[s][:], in_=H_rows[s])
+            if s == 3:
+                nc.sync.dma_start(out=u_rows[:], in_=U.rearrange("(p t) c -> p t c", t=PACK))
+                nc.sync.dma_start(out=v_rows[:], in_=V.rearrange("(h p t) r -> p h t r", p=P, t=PACK))
+        nc.sync.dma_start(out=h_first[1][:], in_=H_rows[0][:, :, W:C2])
+        nc.sync.dma_start(out=a_rows[:], in_=A.rearrange("(p t) c -> p t c", t=PACK))
+        nc.sync.dma_start(out=e_bf[:], in_=e.rearrange("(p t) -> p t", t=PACK))
+        nc.sync.dma_start(out=g_spread[:], in_=g.partition_broadcast(P))
+
+        units = []
+        for s in range(PASSES):
+            units += [("f", 0, [s]), ("h", 0, [s])]
+        units += [("h", 1, [s, s + 1]) for s in range(0, PASSES, 2)]
+        units += [("h", 2, [s, s + 1]) for s in range(0, PASSES - 2, 2)]
+        units += [("h", 2, [PASSES - 2]), ("h", 2, [PASSES - 1])]
+
+        wide, grouped, mx = {}, {}, {}
+
+        def byte_planes(kind, s, chunk):
+            start, width = CHUNKS[chunk]
+            if kind == "f":
+                return f_bytes[s][:]
+            if s == 0:
+                return h_first[start // W][:, :, start % W : start % W + width]
+            return h_bytes[s][:, :, start : start + width]
+
+        def widen(i, on_vector):
+            kind, chunk, passes = units[i]
+            width = CHUNKS[chunk][1]
+            scale = f_scale if kind == "f" else h_scale
+            if i not in wide:
+                wide[i] = stage.tile([P, len(passes), PACK, width], BF16, name="wide", bufs=6)
+            planes = [(n, s, t) for n, s in enumerate(passes) for t in range(PACK)]
+            cut = VECTOR_PLANES.get(i, 0)
+            for n, s, t in planes[:cut] if on_vector else planes[cut:]:
+                plane = byte_planes(kind, s, chunk)[:, t, :].bitcast(FP8)
+                if on_vector:
+                    nc.vector.tensor_scalar(out=wide[i][:, n, t, :], in0=plane, scalar1=scale[:, s, t : t + 1], scalar2=None, op0=MULT)
+                else:
+                    nc.scalar.activation(out=wide[i][:, n, t, :], in_=plane, func=COPY, scale=scale[:, s, t : t + 1])
+
+        def new_grouped(key, columns):
+            grouped[key] = stage.tile([P, columns * PACK], BF16, name="grouped", align_bytes=64, bufs=4)
+            return grouped[key]
+
+        def interleave(key, planes, permute=False):
+            count, width = planes.shape[1], planes.shape[3]
+            target = new_grouped(key, count * width)
+            if permute:
+                dst = target[:].rearrange("p (t m i j) -> p m j i t", t=PACK, i=2, j=PACK)
+                src = planes.rearrange("p n j (m i t) -> p (n m) j i t", i=2, t=PACK)
+            else:
+                dst = target[:].rearrange("p (n c i j) -> p n c j i", n=count, i=4, j=PACK)
+                src = planes.rearrange("p n j (c i) -> p n c j i", i=4)
+            nc.vector.tensor_copy(out=dst, in_=src)
+
+        woven = {}
+
+        def weave(i):
+            src = wide[i][:, 0].rearrange("p j c -> p c j")
+            for b in range(2):
+                woven[i, b] = bank(PACK + 2 * ((i // 2) % 2) + b, [P, 2, W], "woven", BF16)
+                for q in range(2):
+                    nc.tensor.matmul(woven[i, b][:, q, :], lhsT=ident_bf[:], rhs=src[:, (2 * b + q) * P : (2 * b + q + 1) * P, :], start=True, stop=True)
+
+        def weave_out(i):
+            target = new_grouped(i, W)
+            for b in range(2):
+                nc.scalar.copy(out=target[:, b * 2 * W : (b + 1) * 2 * W], in_=woven[i, b][:].rearrange("p q c -> p (q c)"))
+
+        def quantize(key, part=None):
+            columns = grouped[key].shape[1] // PACK
+            if key not in mx:
+                if isinstance(key, int) and units[key][0] == "h":
+                    mx[key] = (stage.tile([P, columns], U32, name="h_codes", align_bytes=64, bufs=4),
+                               stage.tile([P, columns], U8, name="h_scales", align_bytes=64, bufs=4))
+                else:
+                    mx[key] = (keep.tile([P, columns], U32, name="codes_%s" % key, align_bytes=64),
+                               keep.tile([P, columns], U8, name="scales_%s" % key, align_bytes=64))
+            codes, scales = mx[key]
+            lo, hi = (0, columns) if part is None else part
+            nc.vector.quantize_mx(out=codes[:, lo:hi].bitcast(FP8X4), scales=scales[:, lo:hi], in_=grouped[key][:, lo * PACK : hi * PACK])
+
+        def matmul(out, left, t, right, cols, start, stop):
+            rows = slice(t * P, (t + 1) * P)
+            nc.tensor.matmul_mx(
+                out=out, lhsT=mx[left][0][:, rows].bitcast(FP8X4), lhsT_scale=mx[left][1][:, rows],
+                rhs=mx[right][0][:, cols].bitcast(FP8X4), rhs_scale=mx[right][1][:, cols], start=start, stop=stop)
+
+        gram = {}
+
+        def gram_passes(i):
+            kind, chunk, passes = units[i]
+            width = CHUNKS[chunk][1]
+            for n, s in enumerate(passes):
+                for t in range(PACK):
+                    if s == 0:
+                        gram[chunk, t] = bank(PACK * (chunk % 2) + t, [P, width], "gram")
+                    matmul(gram[chunk, t][:], 2 * s, t, i, slice(n * width, (n + 1) * width), s == 0, s == PASSES - 1)
+
+        turned = {}
+
+        def turn(key, rows, t, b):
+            turned[key, t] = bank(b, [P, 2, P], "turned")
+            words = rows[:, t, :].bitcast(F32)
+            for u in range(2):
+                nc.tensor.transpose(turned[key, t][:, u, :], words[:, u::2], ident[:])
+
+        def turn_out(key, t):
+            if t == 0:
+                grouped[key] = keep.tile([P, W * PACK], BF16, name="turned_" + key, align_bytes=64)
+            dst = grouped[key][:, t * W : (t + 1) * W].bitcast(F32).rearrange("p (r u) -> p r u", u=2)
+            nc.scalar.copy(out=dst, in_=turned[key, t][:].rearrange("p u r -> p r u"))
+
+        d, de = {}, {}
+        dg = keep.tile([P, PACK, C2], BF16, name="dg")
+
+        def make_d(chunk, t):
+            start, width = CHUNKS[chunk]
+            if t == 0:
+                d[chunk] = keep.tile([P, PACK, width], F32, name="d%d" % chunk)
+                de[chunk] = keep.tile([P, 1, PACK, width], BF16, name="de%d" % chunk)
+            nc.vector.scalar_tensor_tensor(
+                out=d[chunk][:, t, :], in0=gram[chunk, t][:], scalar=1.0 / PIXELS,
+                in1=a_rows[:, t, start : start + width], op0=MULT, op1=SUBTRACT)
+
+        def make_de(chunk, t):
+            nc.scalar.activation(out=de[chunk][:, 0, t, :], in_=d[chunk][:, t, :], func=COPY, scale=e_col[:, t : t + 1])
+
+        def make_dg(chunk, t):
+            start, width = CHUNKS[chunk]
+            nc.vector.tensor_tensor(out=dg[:, t, start : start + width], in0=d[chunk][:, t, :], in1=g_spread[:, start : start + width], op=MULT)
+
+        Y_rows = out_0.rearrange("(p t) r -> p t r", t=PACK)
+        Z_rows = out_1.rearrange("(p t) c -> p t c", t=PACK)
+        acc = {}
+
+        def z_matmuls(chunk, ts, b):
+            width = CHUNKS[chunk][1]
+            acc["z", chunk, ts[0]] = bank(b, [P, len(ts), width], "z_acc")
+            for n, t in enumerate(ts):
+                matmul(acc["z", chunk, ts[0]][:, n, :], "u", t, "de%d" % chunk, slice(0, width), True, True)
+
+        def y_matmul(t, half):
+            if half == 0:
+                acc["y", 0, t] = bank(PACK + (t + 2) % PACK, [P, 1, R], "y_acc")
+            matmul(acc["y", 0, t][:, 0, :], "dg%d" % half, t, "v%d" % half, slice(0, R), half == 0, half == HALVES - 1)
+
+        def store(which, chunk, t, on_vector):
+            source = acc[which, chunk, t]
+            count, width = source.shape[1], source.shape[2]
+            result = stage.tile([P, count, width], F32, name="result", bufs=6)
+            if on_vector:
+                nc.vector.tensor_copy(out=result[:], in_=source[:])
+            else:
+                nc.scalar.copy(out=result[:], in_=source[:])
+            if which == "y":
+                nc.sync.dma_start(out=Y_rows[:, t : t + 1, :], in_=result[:])
+            else:
+                start = CHUNKS[chunk][0]
+                nc.sync.dma_start(out=Z_rows[:, t : t + count, start : start + width], in_=result[:])
+
+        def extras(i):
+            if i == 8:
+                interleave("v0", v_rows[:, 0:1])
+            if i == 10:
+                quantize("v0")
+            if i == 12:
+                interleave("v1", v_rows[:, 1:2])
+            if i == 14:
+                quantize("v1")
+                nc.vector.tensor_copy(out=e_col[:], in_=e_bf[:])
+            if i == 16:
+                for t in range(PACK):
+                    turn("u", u_rows, t, PACK + t)
+                for t in range(PACK):
+                    turn_out("u", t)
+            if i == 17:
+                for t in range(PACK):
+                    make_d(0, t)
+                    make_de(0, t)
+                quantize("u")
+            if i == 18:
+                for t in range(PACK):
+                    make_dg(0, t)
+                    turn("dg0", dg[:, :, 0:W], t, t)
+                for t in range(PACK):
+                    turn_out("dg0", t)
+            if i == 19:
+                interleave("de0", de[0][:])
+            if i == 20:
+                quantize("de0")
+                for t in range(PACK):
+                    z_matmuls(0, [t], t)
+                for t in range(PACK):
+                    store("z", 0, t, False)
+            if i == 21:
+                for t in range(PACK):
+                    make_d(1, t)
+                    make_de(1, t)
+            if i == 22:
+                quantize("dg0")
+                y_matmul(0, 0)
+                y_matmul(1, 0)
+                interleave("de1", de[1][:])
+            if i == 23:
+                quantize("de1")
+                for pair in range(2):
+                    z_matmuls(1, [2 * pair, 2 * pair + 1], PACK + pair)
+                for pair in range(2):
+                    store("z", 1, 2 * pair, False)
+
+        n_units = len(units)
+        widen(0, True)
+        widen(0, False)
+        widen(1, False)
+        for i in range(n_units + 1):
+            if i + 2 < n_units:
+                widen(i + 2, False)
+            if i + 1 < n_units:
+                widen(i + 1, True)
+                if i + 1 in TENSOR_UNITS:
+                    weave(i + 1)
+            if i < n_units:
+                if i in TENSOR_UNITS:
+                    weave_out(i)
+                else:
+                    interleave(i, wide[i][:], permute=units[i][0] == "f")
+            extras(i)
+            if i >= 1:
+                quantize(i - 1)
+                if units[i - 1][0] == "h":
+                    gram_passes(i - 1)
+
+        last = len(CHUNKS) - 1
+        y_matmul(2, 0)
+        y_matmul(3, 0)
+        for t in range(PACK):
+            make_dg(last - 1, t)
+        for pair in range(2):
+            for t in (2 * pair, 2 * pair + 1):
+                make_d(last, t)
+            for t in (2 * pair, 2 * pair + 1):
+                make_dg(last, t)
+                turn("dg1", dg[:, :, W:C2], t, t)
+            for t in (2 * pair, 2 * pair + 1):
+                make_de(last, t)
+            for t in (2 * pair, 2 * pair + 1):
+                turn_out("dg1", t)
+        quantize("dg1", (0, 2 * P))
+        y_matmul(0, 1)
+        y_matmul(1, 1)
+        interleave("de2", de[last][:])
+        quantize("dg1", (2 * P, 4 * P))
+        y_matmul(2, 1)
+        y_matmul(3, 1)
+        store("y", 0, 0, False)
+        quantize("de2")
+        for pair in range(2):
+            z_matmuls(last, [2 * pair, 2 * pair + 1], pair)
+        store("y", 0, 1, True)
+        store("y", 0, 2, False)
+        store("y", 0, 3, True)
+        store("z", last, 0, False)
+        store("z", last, 2, True)

@@ -22,9 +22,11 @@ W = 512
 PASSES = PIXELS // W
 HALVES = C2 // W
 
-CHUNKS = [(0, 512), (512, 256), (768, 256)]
-VECTOR_PLANES = {0: 2, 1: 3, 2: 4, 4: 3, 6: 4, 8: 3, 10: 3, 12: 3, 14: 3, 16: 2}
-TENSOR_UNITS = {3, 5, 7, 9, 11, 13, 15}
+F_ON_SCALAR = {2: 1, 3: 1, 4: 1, 5: 1}
+H_ON_VECTOR = {0: 2}
+U_PERIOD = 5
+V_PERIODS = [6, 7]
+WEAVE_BANKS = (6, 7)
 
 
 def tile_cross_layer_gram_sketch_d5_kernel(tc, F_bytes, F_scale, H_bytes, H_scale, A, g, e, V, U, out_0, out_1):
@@ -38,10 +40,13 @@ def tile_cross_layer_gram_sketch_d5_kernel(tc, F_bytes, F_scale, H_bytes, H_scal
         def bank(b, shape, name, dtype=F32):
             return psum.tile(shape, dtype, name=name, tag="bank%d" % b)
 
-        f_scale = keep.tile([P, PASSES, PACK], F32, name="f_scale")
-        h_scale = keep.tile([P, PASSES, PACK], F32, name="h_scale")
-        nc.scalar.dma_start(out=f_scale[:], in_=F_scale.rearrange("(s p t) o -> p s (t o)", p=P, t=PACK))
-        nc.scalar.dma_start(out=h_scale[:], in_=H_scale.rearrange("(s p t) o -> p s (t o)", p=P, t=PACK))
+        scale_rows = {"f": F_scale.rearrange("(s p t) o -> p s (t o)", p=P, t=PACK), "h": H_scale.rearrange("(s p t) o -> p s (t o)", p=P, t=PACK)}
+        scale_first = {kind: keep.tile([P, 1, PACK], F32, name=kind + "_scale_first") for kind in "hf"}
+        scale_rest = {kind: keep.tile([P, PASSES - 1, PACK], F32, name=kind + "_scale_rest") for kind in "hf"}
+        for kind in "hf":
+            nc.scalar.dma_start(out=scale_first[kind][:], in_=scale_rows[kind][:, 0:1, :])
+        for kind in "hf":
+            nc.scalar.dma_start(out=scale_rest[kind][:], in_=scale_rows[kind][:, 1:PASSES, :])
         warm_in = keep.tile([P, 1], F32, name="warm_in")
         warm_out = keep.tile([P, 1], F32, name="warm_out")
         nc.vector.memset(warm_in[:], 0.0)
@@ -55,8 +60,7 @@ def tile_cross_layer_gram_sketch_d5_kernel(tc, F_bytes, F_scale, H_bytes, H_scal
         F_rows = F_bytes.rearrange("(s p t) c -> s p t c", p=P, t=PACK)
         H_rows = H_bytes.rearrange("(s p t) c -> s p t c", p=P, t=PACK)
         f_bytes = [keep.tile([P, PACK, C1], U8, name="f_bytes%d" % s) for s in range(PASSES)]
-        h_bytes = [None] + [keep.tile([P, PACK, C2], U8, name="h_bytes%d" % s) for s in range(1, PASSES)]
-        h_first = [keep.tile([P, PACK, W], U8, name="h_bytes0_%d" % half) for half in range(HALVES)]
+        h_bytes = [keep.tile([P, PACK, C2], U8, name="h_bytes%d" % s) for s in range(PASSES)]
         u_rows = keep.tile([P, PACK, C1], BF16, name="u_rows")
         v_rows = keep.tile([P, HALVES, PACK, R], BF16, name="v_rows")
         a_rows = keep.tile([P, PACK, C2], BF16, name="a_rows")
@@ -64,273 +68,273 @@ def tile_cross_layer_gram_sketch_d5_kernel(tc, F_bytes, F_scale, H_bytes, H_scal
         e_col = keep.tile([P, PACK], F32, name="e_col")
         g_spread = keep.tile([P, C2], BF16, name="g_spread")
 
+        nc.sync.dma_start(out=h_bytes[0][:, 2:3, :], in_=H_rows[0][:, 2:3, :])
         nc.sync.dma_start(out=f_bytes[0][:, 0:2, :], in_=F_rows[0][:, 0:2, :])
+        nc.sync.dma_start(out=h_bytes[0][:, 3:4, :], in_=H_rows[0][:, 3:4, :])
         nc.sync.dma_start(out=f_bytes[0][:, 2:4, :], in_=F_rows[0][:, 2:4, :])
-        nc.sync.dma_start(out=h_first[0][:], in_=H_rows[0][:, :, 0:W])
+        nc.sync.dma_start(out=h_bytes[0][:, 0:2, :], in_=H_rows[0][:, 0:2, :])
         for s in range(1, PASSES):
-            nc.sync.dma_start(out=f_bytes[s][:], in_=F_rows[s])
             nc.sync.dma_start(out=h_bytes[s][:], in_=H_rows[s])
-            if s == 3:
-                nc.sync.dma_start(out=u_rows[:], in_=U.rearrange("(p t) c -> p t c", t=PACK))
-                nc.sync.dma_start(out=v_rows[:], in_=V.rearrange("(h p t) r -> p h t r", p=P, t=PACK))
-        nc.sync.dma_start(out=h_first[1][:], in_=H_rows[0][:, :, W:C2])
+            nc.sync.dma_start(out=f_bytes[s][:], in_=F_rows[s])
+        nc.sync.dma_start(out=u_rows[:], in_=U.rearrange("(p t) c -> p t c", t=PACK))
+        nc.sync.dma_start(out=v_rows[:], in_=V.rearrange("(h p t) r -> p h t r", p=P, t=PACK))
         nc.sync.dma_start(out=a_rows[:], in_=A.rearrange("(p t) c -> p t c", t=PACK))
         nc.sync.dma_start(out=e_bf[:], in_=e.rearrange("(p t) -> p t", t=PACK))
         nc.sync.dma_start(out=g_spread[:], in_=g.partition_broadcast(P))
 
-        units = []
-        for s in range(PASSES):
-            units += [("f", 0, [s]), ("h", 0, [s])]
-        units += [("h", 1, [s, s + 1]) for s in range(0, PASSES, 2)]
-        units += [("h", 2, [s, s + 1]) for s in range(0, PASSES - 2, 2)]
-        units += [("h", 2, [PASSES - 2]), ("h", 2, [PASSES - 1])]
-
         wide, grouped, mx = {}, {}, {}
 
-        def byte_planes(kind, s, chunk):
-            start, width = CHUNKS[chunk]
-            if kind == "f":
-                return f_bytes[s][:]
-            if s == 0:
-                return h_first[start // W][:, :, start % W : start % W + width]
-            return h_bytes[s][:, :, start : start + width]
+        def wide_tile(key, shape, dtype, tag):
+            if key not in wide:
+                wide[key] = stage.tile(shape, dtype, name=tag, tag=tag)
+            return wide[key]
 
-        def widen(i, on_vector):
-            kind, chunk, passes = units[i]
-            width = CHUNKS[chunk][1]
-            scale = f_scale if kind == "f" else h_scale
-            if i not in wide:
-                wide[i] = stage.tile([P, len(passes), PACK, width], BF16, name="wide", bufs=6)
-            planes = [(n, s, t) for n, s in enumerate(passes) for t in range(PACK)]
-            cut = VECTOR_PLANES.get(i, 0)
-            for n, s, t in planes[:cut] if on_vector else planes[cut:]:
-                plane = byte_planes(kind, s, chunk)[:, t, :].bitcast(FP8)
-                if on_vector:
-                    nc.vector.tensor_scalar(out=wide[i][:, n, t, :], in0=plane, scalar1=scale[:, s, t : t + 1], scalar2=None, op0=MULT)
-                else:
-                    nc.scalar.activation(out=wide[i][:, n, t, :], in_=plane, func=COPY, scale=scale[:, s, t : t + 1])
-
-        def new_grouped(key, columns):
-            grouped[key] = stage.tile([P, columns * PACK], BF16, name="grouped", align_bytes=64, bufs=4)
-            return grouped[key]
-
-        def interleave(key, planes, permute=False):
-            count, width = planes.shape[1], planes.shape[3]
-            target = new_grouped(key, count * width)
-            if permute:
-                dst = target[:].rearrange("p (t m i j) -> p m j i t", t=PACK, i=2, j=PACK)
-                src = planes.rearrange("p n j (m i t) -> p (n m) j i t", i=2, t=PACK)
+        def widen(kind, s, t, on_vector, cols=None):
+            source = f_bytes if kind == "f" else h_bytes
+            scale = scale_first[kind][:, 0, t : t + 1] if s == 0 else scale_rest[kind][:, s - 1, t : t + 1]
+            width = source[s].shape[2]
+            cols = slice(0, width) if cols is None else cols
+            target = wide_tile((kind, s), [P, PACK, width], BF16, "wide_" + kind)
+            plane = source[s][:, t, cols].bitcast(FP8)
+            if on_vector:
+                nc.vector.tensor_scalar(out=target[:, t, cols], in0=plane, scalar1=scale, scalar2=None, op0=MULT)
             else:
-                dst = target[:].rearrange("p (n c i j) -> p n c j i", n=count, i=4, j=PACK)
-                src = planes.rearrange("p n j (c i) -> p n c j i", i=4)
-            nc.vector.tensor_copy(out=dst, in_=src)
+                nc.scalar.activation(out=target[:, t, cols], in_=plane, func=COPY, scale=scale)
+
+        def group_tile(key, slots, names):
+            tag = "grouped%d" % slots
+            tile = stage.tile([P, slots * W * PACK], BF16, name=tag, tag=tag, align_bytes=64, bufs=5 - slots)
+            grouped[key] = (tile, names)
+            for n, name in enumerate(names):
+                grouped[name] = tile[:, n * W * PACK : (n + 1) * W * PACK]
+
+        def interleave(name, planes, permute=False, on_scalar=False):
+            if permute:
+                dst = grouped[name].rearrange("p (t m i j) -> p m j i t", t=PACK, i=2, j=PACK)
+                src = planes.rearrange("p j (m i t) -> p m j i t", i=2, t=PACK)
+            else:
+                dst = grouped[name].rearrange("p (c i j) -> p c j i", i=4, j=PACK)
+                src = planes.rearrange("p j (c i) -> p c j i", i=4)
+            if on_scalar:
+                nc.scalar.copy(out=dst, in_=src)
+            else:
+                nc.vector.tensor_copy(out=dst, in_=src)
 
         woven = {}
 
-        def weave(i):
-            src = wide[i][:, 0].rearrange("p j c -> p c j")
+        def weave(s):
+            src = wide["h", s][:, :, 0:W].rearrange("p j c -> p c j")
             for b in range(2):
-                woven[i, b] = bank(PACK + 2 * ((i // 2) % 2) + b, [P, 2, W], "woven", BF16)
+                woven[b] = bank(WEAVE_BANKS[b], [P, 2, W], "woven", BF16)
                 for q in range(2):
-                    nc.tensor.matmul(woven[i, b][:, q, :], lhsT=ident_bf[:], rhs=src[:, (2 * b + q) * P : (2 * b + q + 1) * P, :], start=True, stop=True)
+                    nc.tensor.matmul(woven[b][:, q, :], lhsT=ident_bf[:], rhs=src[:, (2 * b + q) * P : (2 * b + q + 1) * P, :], start=True, stop=True)
 
-        def weave_out(i):
-            target = new_grouped(i, W)
+        def weave_out(s):
             for b in range(2):
-                nc.scalar.copy(out=target[:, b * 2 * W : (b + 1) * 2 * W], in_=woven[i, b][:].rearrange("p q c -> p (q c)"))
+                nc.scalar.copy(out=grouped["h%d_0" % s][:, b * 2 * W : (b + 1) * 2 * W], in_=woven[b][:].rearrange("p q c -> p (q c)"))
 
-        def quantize(key, part=None):
-            columns = grouped[key].shape[1] // PACK
+        def quantize(key, part=None, transient=False):
+            tile, names = grouped[key]
+            columns = len(names) * W
             if key not in mx:
-                if isinstance(key, int) and units[key][0] == "h":
-                    mx[key] = (stage.tile([P, columns], U32, name="h_codes", align_bytes=64, bufs=4),
-                               stage.tile([P, columns], U8, name="h_scales", align_bytes=64, bufs=4))
+                if transient:
+                    mx[key] = (stage.tile([P, columns], U32, name="h_codes", align_bytes=64),
+                               stage.tile([P, columns], U8, name="h_scales", align_bytes=64))
                 else:
-                    mx[key] = (keep.tile([P, columns], U32, name="codes_%s" % key, align_bytes=64),
-                               keep.tile([P, columns], U8, name="scales_%s" % key, align_bytes=64))
+                    mx[key] = (keep.tile([P, columns], U32, name="codes_" + key, align_bytes=64),
+                               keep.tile([P, columns], U8, name="scales_" + key, align_bytes=64))
+                for n, name in enumerate(names):
+                    mx[name] = (mx[key][0][:, n * W : (n + 1) * W], mx[key][1][:, n * W : (n + 1) * W])
             codes, scales = mx[key]
             lo, hi = (0, columns) if part is None else part
-            nc.vector.quantize_mx(out=codes[:, lo:hi].bitcast(FP8X4), scales=scales[:, lo:hi], in_=grouped[key][:, lo * PACK : hi * PACK])
+            nc.vector.quantize_mx(out=codes[:, lo:hi].bitcast(FP8X4), scales=scales[:, lo:hi], in_=tile[:, lo * PACK : hi * PACK])
 
-        def matmul(out, left, t, right, cols, start, stop):
+        def matmul(out, left, t, right, start, stop):
             rows = slice(t * P, (t + 1) * P)
             nc.tensor.matmul_mx(
                 out=out, lhsT=mx[left][0][:, rows].bitcast(FP8X4), lhsT_scale=mx[left][1][:, rows],
-                rhs=mx[right][0][:, cols].bitcast(FP8X4), rhs_scale=mx[right][1][:, cols], start=start, stop=stop)
+                rhs=mx[right][0].bitcast(FP8X4), rhs_scale=mx[right][1], start=start, stop=stop)
 
         gram = {}
 
-        def gram_passes(i):
-            kind, chunk, passes = units[i]
-            width = CHUNKS[chunk][1]
-            for n, s in enumerate(passes):
-                for t in range(PACK):
-                    if s == 0:
-                        gram[chunk, t] = bank(PACK * (chunk % 2) + t, [P, width], "gram")
-                    matmul(gram[chunk, t][:], 2 * s, t, i, slice(n * width, (n + 1) * width), s == 0, s == PASSES - 1)
+        def gram_pass(s, half, t):
+            if s == 0:
+                gram[half, t] = bank(PACK * half + t, [P, W], "gram")
+            matmul(gram[half, t][:], "f%d" % s, t, "h%d_%d" % (s, half), s == 0, s == PASSES - 1)
 
         turned = {}
 
-        def turn(key, rows, t, b):
-            turned[key, t] = bank(b, [P, 2, P], "turned")
-            words = rows[:, t, :].bitcast(F32)
-            for u in range(2):
-                nc.tensor.transpose(turned[key, t][:, u, :], words[:, u::2], ident[:])
+        def turn(name, rows, first, count, b):
+            turned[name, first] = bank(b, [P, count, 2, P], "turned")
+            for j in range(count):
+                words = rows[:, first + j, :].bitcast(F32)
+                for u in range(2):
+                    nc.tensor.transpose(turned[name, first][:, j, u, :], words[:, u::2], ident[:])
 
-        def turn_out(key, t):
-            if t == 0:
-                grouped[key] = keep.tile([P, W * PACK], BF16, name="turned_" + key, align_bytes=64)
-            dst = grouped[key][:, t * W : (t + 1) * W].bitcast(F32).rearrange("p (r u) -> p r u", u=2)
-            nc.scalar.copy(out=dst, in_=turned[key, t][:].rearrange("p u r -> p r u"))
+        def turn_out(name, first, count):
+            dst = grouped[name][:, first * W : (first + count) * W].bitcast(F32).rearrange("p (j r u) -> p j r u", j=count, u=2)
+            nc.scalar.copy(out=dst, in_=turned[name, first][:].rearrange("p j u r -> p j r u"))
+
+        last = PASSES - 1
+        for k in range(PASSES):
+            first_plane = H_ON_VECTOR.get(k, 0)
+            on_scalar = F_ON_SCALAR.get(k + 1, 0)
+            for t in range(first_plane, max(first_plane, 2)):
+                widen("h", k, t, False, slice(0, W) if k == last else None)
+            if k >= 1:
+                group_tile("a%d" % (k - 1), 1, ["h%d_0" % (k - 1)])
+                weave_out(k - 1)
+            if k == U_PERIOD:
+                group_tile("ug", 1, ["u"])
+                for pair in range(2):
+                    turn("u", u_rows, 2 * pair, 2, WEAVE_BANKS[pair])
+            if k < last:
+                for t in range(max(first_plane, 2), PACK):
+                    widen("h", k, t, False)
+                if k == U_PERIOD:
+                    for pair in range(2):
+                        turn_out("u", 2 * pair, 2)
+                for t in range(on_scalar):
+                    widen("f", k + 1, t, False)
+            else:
+                for t in range(2, PACK):
+                    widen("h", k, t, False, slice(0, W))
+                for t in range(PACK):
+                    widen("h", k, t, False, slice(W, C2))
+            if k == 0:
+                for t in range(PACK):
+                    widen("f", 0, t, True)
+                for t in range(first_plane):
+                    widen("h", 0, t, True)
+            if k < last:
+                weave(k)
+            else:
+                for t in range(2, PACK):
+                    for s in range(last - 1):
+                        gram_pass(s, 1, t)
+            names = ["f%d" % k] + (["h%d_1" % (k - 1)] if k >= 1 else [])
+            group_tile("b%d" % k, 2, names)
+            interleave("f%d" % k, wide["f", k][:], permute=True)
+            if k >= 1:
+                interleave("h%d_1" % (k - 1), wide["h", k - 1][:, :, W:C2])
+            if k < last:
+                for t in range(on_scalar, PACK):
+                    widen("f", k + 1, t, True)
+            if k == U_PERIOD + 1:
+                quantize("ug")
+                nc.vector.tensor_copy(out=e_col[:], in_=e_bf[:])
+            if k in V_PERIODS:
+                if k == V_PERIODS[0]:
+                    group_tile("v", 2, ["v0", "v1"])
+                interleave("v%d" % V_PERIODS.index(k), v_rows[:, V_PERIODS.index(k)])
+            if k >= 1:
+                quantize("a%d" % (k - 1), transient=True)
+            quantize("b%d" % k)
+            if k >= 1:
+                for t in range(PACK):
+                    gram_pass(k - 1, 0, t)
+                for t in range(PACK if k == last else 2):
+                    gram_pass(k - 1, 1, t)
 
         d, de = {}, {}
-        dg = keep.tile([P, PACK, C2], BF16, name="dg")
+        dg = wide_tile("dg", [P, PACK, C2], BF16, "wide_h")
 
-        def make_d(chunk, t):
-            start, width = CHUNKS[chunk]
-            if t == 0:
-                d[chunk] = keep.tile([P, PACK, width], F32, name="d%d" % chunk)
-                de[chunk] = keep.tile([P, 1, PACK, width], BF16, name="de%d" % chunk)
+        def make_d(half, t):
+            d[half] = wide_tile(("d", half), [P, PACK, W], F32, "wide_h")
             nc.vector.scalar_tensor_tensor(
-                out=d[chunk][:, t, :], in0=gram[chunk, t][:], scalar=1.0 / PIXELS,
-                in1=a_rows[:, t, start : start + width], op0=MULT, op1=SUBTRACT)
+                out=d[half][:, t, :], in0=gram[half, t][:], scalar=1.0 / PIXELS,
+                in1=a_rows[:, t, half * W : (half + 1) * W], op0=MULT, op1=SUBTRACT)
 
-        def make_de(chunk, t):
-            nc.scalar.activation(out=de[chunk][:, 0, t, :], in_=d[chunk][:, t, :], func=COPY, scale=e_col[:, t : t + 1])
+        def make_de(half, t):
+            de[half] = wide_tile(("de", half), [P, PACK, W], BF16, "wide_f")
+            nc.scalar.activation(out=de[half][:, t, :], in_=d[half][:, t, :], func=COPY, scale=e_col[:, t : t + 1])
 
-        def make_dg(chunk, t):
-            start, width = CHUNKS[chunk]
-            nc.vector.tensor_tensor(out=dg[:, t, start : start + width], in0=d[chunk][:, t, :], in1=g_spread[:, start : start + width], op=MULT)
+        def make_dg(half, first, count):
+            cols = slice(half * W, (half + 1) * W)
+            ts = slice(first, first + count)
+            nc.vector.tensor_tensor(out=dg[:, ts, cols], in0=d[half][:, ts, :], in1=g_spread[:, cols].unsqueeze(1).to_broadcast([P, count, W]), op=MULT)
 
         Y_rows = out_0.rearrange("(p t) r -> p t r", t=PACK)
         Z_rows = out_1.rearrange("(p t) c -> p t c", t=PACK)
         acc = {}
 
-        def z_matmuls(chunk, ts, b):
-            width = CHUNKS[chunk][1]
-            acc["z", chunk, ts[0]] = bank(b, [P, len(ts), width], "z_acc")
-            for n, t in enumerate(ts):
-                matmul(acc["z", chunk, ts[0]][:, n, :], "u", t, "de%d" % chunk, slice(0, width), True, True)
+        def z_matmul(half, t, b):
+            acc["z", half, t] = bank(b, [P, W], "z_acc")
+            matmul(acc["z", half, t][:], "u", t, "de%d" % half, True, True)
 
-        def y_matmul(t, half):
+        def y_matmul(t, half, b):
             if half == 0:
-                acc["y", 0, t] = bank(PACK + (t + 2) % PACK, [P, 1, R], "y_acc")
-            matmul(acc["y", 0, t][:, 0, :], "dg%d" % half, t, "v%d" % half, slice(0, R), half == 0, half == HALVES - 1)
+                acc["y", 0, t] = bank(b, [P, R], "y_acc")
+            matmul(acc["y", 0, t][:], "dg%d" % half, t, "v%d" % half, half == 0, half == HALVES - 1)
 
-        def store(which, chunk, t, on_vector):
-            source = acc[which, chunk, t]
-            count, width = source.shape[1], source.shape[2]
-            result = stage.tile([P, count, width], F32, name="result", bufs=6)
+        def store(which, half, t, on_vector):
+            result = stage.tile([P, W], F32, name="result", bufs=8)
             if on_vector:
-                nc.vector.tensor_copy(out=result[:], in_=source[:])
+                nc.vector.tensor_copy(out=result[:], in_=acc[which, half, t][:])
             else:
-                nc.scalar.copy(out=result[:], in_=source[:])
-            if which == "y":
-                nc.sync.dma_start(out=Y_rows[:, t : t + 1, :], in_=result[:])
-            else:
-                start = CHUNKS[chunk][0]
-                nc.sync.dma_start(out=Z_rows[:, t : t + count, start : start + width], in_=result[:])
+                nc.scalar.copy(out=result[:], in_=acc[which, half, t][:])
+            rows = Y_rows if which == "y" else Z_rows
+            nc.sync.dma_start(out=rows[:, t, half * W : (half + 1) * W], in_=result[:])
 
-        def extras(i):
-            if i == 8:
-                interleave("v0", v_rows[:, 0:1])
-            if i == 10:
-                quantize("v0")
-            if i == 12:
-                interleave("v1", v_rows[:, 1:2])
-            if i == 14:
-                quantize("v1")
-                nc.vector.tensor_copy(out=e_col[:], in_=e_bf[:])
-            if i == 16:
-                for t in range(PACK):
-                    turn("u", u_rows, t, PACK + t)
-                for t in range(PACK):
-                    turn_out("u", t)
-            if i == 17:
-                for t in range(PACK):
-                    make_d(0, t)
-                    make_de(0, t)
-                quantize("u")
-            if i == 18:
-                for t in range(PACK):
-                    make_dg(0, t)
-                    turn("dg0", dg[:, :, 0:W], t, t)
-                for t in range(PACK):
-                    turn_out("dg0", t)
-            if i == 19:
-                interleave("de0", de[0][:])
-            if i == 20:
-                quantize("de0")
-                for t in range(PACK):
-                    z_matmuls(0, [t], t)
-                for t in range(PACK):
-                    store("z", 0, t, False)
-            if i == 21:
-                for t in range(PACK):
-                    make_d(1, t)
-                    make_de(1, t)
-            if i == 22:
-                quantize("dg0")
-                y_matmul(0, 0)
-                y_matmul(1, 0)
-                interleave("de1", de[1][:])
-            if i == 23:
-                quantize("de1")
-                for pair in range(2):
-                    z_matmuls(1, [2 * pair, 2 * pair + 1], PACK + pair)
-                for pair in range(2):
-                    store("z", 1, 2 * pair, False)
-
-        n_units = len(units)
-        widen(0, True)
-        widen(0, False)
-        widen(1, False)
-        for i in range(n_units + 1):
-            if i + 2 < n_units:
-                widen(i + 2, False)
-            if i + 1 < n_units:
-                widen(i + 1, True)
-                if i + 1 in TENSOR_UNITS:
-                    weave(i + 1)
-            if i < n_units:
-                if i in TENSOR_UNITS:
-                    weave_out(i)
-                else:
-                    interleave(i, wide[i][:], permute=units[i][0] == "f")
-            extras(i)
-            if i >= 1:
-                quantize(i - 1)
-                if units[i - 1][0] == "h":
-                    gram_passes(i - 1)
-
-        last = len(CHUNKS) - 1
-        y_matmul(2, 0)
-        y_matmul(3, 0)
+        ha, hb = "h%d_0" % last, "h%d_1" % last
+        group_tile("a_last", 1, [ha])
+        interleave(ha, wide["h", last][:, :, 0:W])
+        quantize("v", (0, W))
+        quantize("a_last", transient=True)
         for t in range(PACK):
-            make_dg(last - 1, t)
-        for pair in range(2):
-            for t in (2 * pair, 2 * pair + 1):
-                make_d(last, t)
-            for t in (2 * pair, 2 * pair + 1):
-                make_dg(last, t)
-                turn("dg1", dg[:, :, W:C2], t, t)
-            for t in (2 * pair, 2 * pair + 1):
-                make_de(last, t)
-            for t in (2 * pair, 2 * pair + 1):
-                turn_out("dg1", t)
-        quantize("dg1", (0, 2 * P))
-        y_matmul(0, 1)
-        y_matmul(1, 1)
-        interleave("de2", de[last][:])
-        quantize("dg1", (2 * P, 4 * P))
-        y_matmul(2, 1)
-        y_matmul(3, 1)
-        store("y", 0, 0, False)
-        quantize("de2")
-        for pair in range(2):
-            z_matmuls(last, [2 * pair, 2 * pair + 1], pair)
-        store("y", 0, 1, True)
-        store("y", 0, 2, False)
-        store("y", 0, 3, True)
-        store("z", last, 0, False)
-        store("z", last, 2, True)
+            gram_pass(last, 0, t)
+        group_tile("b_last", 1, [hb])
+        interleave(hb, wide["h", last][:, :, W:C2], on_scalar=True)
+        quantize("v", (W, 2 * W))
+        for t in range(PACK):
+            make_d(0, t)
+            make_de(0, t)
+            if t == 1:
+                quantize("b_last", transient=True)
+                for tt in range(PACK):
+                    gram_pass(last, 1, tt)
+        group_tile("de0g", 1, ["de0"])
+        interleave("de0", de[0][:], on_scalar=True)
+        for t in range(PACK):
+            make_d(1, t)
+            make_de(1, t)
+        group_tile("dgg", 2, ["dg0", "dg1"])
+        make_dg(0, 0, 2)
+        turn("dg0", dg[:, :, 0:W], 0, 2, 0)
+        quantize("de0g")
+        for t in range(3):
+            z_matmul(0, t, 1 + t)
+        make_dg(0, 2, 2)
+        turn("dg0", dg[:, :, 0:W], 2, 2, 4)
+        turn_out("dg0", 0, 2)
+        z_matmul(0, 3, 0)
+        group_tile("de1g", 1, ["de1"])
+        interleave("de1", de[1][:])
+        store("z", 0, 0, False)
+        turn_out("dg0", 2, 2)
+        for t in range(1, PACK):
+            store("z", 0, t, False)
+        make_dg(1, 0, 2)
+        turn("dg1", dg[:, :, W:C2], 0, 2, 1)
+        quantize("de1g")
+        for t in range(PACK):
+            z_matmul(1, t, PACK + (1 + t) % PACK)
+        turn_out("dg1", 0, 2)
+        make_dg(1, 2, 2)
+        turn("dg1", dg[:, :, W:C2], 2, 2, 2)
+        quantize("dgg", (0, W))
+        store("z", 1, 0, False)
+        store("z", 1, 1, False)
+        quantize("dgg", (W, W + 2 * P))
+        for t in range(2):
+            y_matmul(t, 0, t)
+            y_matmul(t, 1, t)
+        turn_out("dg1", 2, 2)
+        store("z", 1, 2, True)
+        quantize("dgg", (W + 2 * P, 2 * W))
+        for t in range(2, PACK):
+            y_matmul(t, 0, t)
+            y_matmul(t, 1, t)
+        store("z", 1, 3, False)
+        for t in range(PACK):
+            store("y", 0, t, t % 2 == 0)

@@ -22,11 +22,15 @@ W = 512
 PASSES = PIXELS // W
 HALVES = C2 // W
 
-F_ON_SCALAR = {2: 1, 3: 1, 4: 1, 5: 1}
+F_ON_SCALAR = {2: 1, 4: 1, 6: 1}
 H_ON_VECTOR = {0: 2}
-U_PERIOD = 5
-V_PERIODS = [6, 7]
+RAW_BUFS = 5
+WIDE_BUFS = {"wide_h": 3, "wide_f": 3}
+U_PERIOD = 1
+V_PERIOD = 5
+TO_AT = 3
 WEAVE_BANKS = (6, 7)
+WOVEN = list(range(PASSES - 1))
 
 
 def tile_cross_layer_gram_sketch_d5_kernel(tc, F_bytes, F_scale, H_bytes, H_scale, A, g, e, V, U, out_0, out_1):
@@ -59,8 +63,15 @@ def tile_cross_layer_gram_sketch_d5_kernel(tc, F_bytes, F_scale, H_bytes, H_scal
 
         F_rows = F_bytes.rearrange("(s p t) c -> s p t c", p=P, t=PACK)
         H_rows = H_bytes.rearrange("(s p t) c -> s p t c", p=P, t=PACK)
-        f_bytes = [keep.tile([P, PACK, C1], U8, name="f_bytes%d" % s) for s in range(PASSES)]
-        h_bytes = [keep.tile([P, PACK, C2], U8, name="h_bytes%d" % s) for s in range(PASSES)]
+        f_bytes, h_bytes = {}, {}
+
+        def load_pass(s, pieces):
+            f_bytes[s] = stage.tile([P, PACK, C1], U8, name="f_bytes", bufs=RAW_BUFS)
+            h_bytes[s] = stage.tile([P, PACK, C2], U8, name="h_bytes", bufs=RAW_BUFS)
+            for kind, lo, hi in pieces:
+                target, rows = (f_bytes, F_rows) if kind == "f" else (h_bytes, H_rows)
+                nc.sync.dma_start(out=target[s][:, lo:hi, :], in_=rows[s][:, lo:hi, :])
+
         u_rows = keep.tile([P, PACK, C1], BF16, name="u_rows")
         v_rows = keep.tile([P, HALVES, PACK, R], BF16, name="v_rows")
         a_rows = keep.tile([P, PACK, C2], BF16, name="a_rows")
@@ -68,15 +79,12 @@ def tile_cross_layer_gram_sketch_d5_kernel(tc, F_bytes, F_scale, H_bytes, H_scal
         e_col = keep.tile([P, PACK], F32, name="e_col")
         g_spread = keep.tile([P, C2], BF16, name="g_spread")
 
-        nc.sync.dma_start(out=h_bytes[0][:, 2:3, :], in_=H_rows[0][:, 2:3, :])
-        nc.sync.dma_start(out=f_bytes[0][:, 0:2, :], in_=F_rows[0][:, 0:2, :])
-        nc.sync.dma_start(out=h_bytes[0][:, 3:4, :], in_=H_rows[0][:, 3:4, :])
-        nc.sync.dma_start(out=f_bytes[0][:, 2:4, :], in_=F_rows[0][:, 2:4, :])
-        nc.sync.dma_start(out=h_bytes[0][:, 0:2, :], in_=H_rows[0][:, 0:2, :])
-        for s in range(1, PASSES):
-            nc.sync.dma_start(out=h_bytes[s][:], in_=H_rows[s])
-            nc.sync.dma_start(out=f_bytes[s][:], in_=F_rows[s])
-        nc.sync.dma_start(out=u_rows[:], in_=U.rearrange("(p t) c -> p t c", t=PACK))
+        whole = [("h", 0, PACK), ("f", 0, PACK)]
+        load_pass(0, [("h", 2, 3), ("f", 0, 2), ("h", 3, 4), ("f", 2, 4), ("h", 0, 2)])
+        for s in range(1, RAW_BUFS):
+            load_pass(s, whole)
+            if s == 2:
+                nc.sync.dma_start(out=u_rows[:], in_=U.rearrange("(p t) c -> p t c", t=PACK))
         nc.sync.dma_start(out=v_rows[:], in_=V.rearrange("(h p t) r -> p h t r", p=P, t=PACK))
         nc.sync.dma_start(out=a_rows[:], in_=A.rearrange("(p t) c -> p t c", t=PACK))
         nc.sync.dma_start(out=e_bf[:], in_=e.rearrange("(p t) -> p t", t=PACK))
@@ -86,30 +94,35 @@ def tile_cross_layer_gram_sketch_d5_kernel(tc, F_bytes, F_scale, H_bytes, H_scal
 
         def wide_tile(key, shape, dtype, tag):
             if key not in wide:
-                wide[key] = stage.tile(shape, dtype, name=tag, tag=tag)
+                wide[key] = stage.tile(shape, dtype, name=tag, tag=tag, bufs=WIDE_BUFS[tag])
             return wide[key]
 
-        def widen(kind, s, t, on_vector, cols=None):
+        def widen(kind, s, t, on_vector, half=None):
             source = f_bytes if kind == "f" else h_bytes
             scale = scale_first[kind][:, 0, t : t + 1] if s == 0 else scale_rest[kind][:, s - 1, t : t + 1]
-            width = source[s].shape[2]
-            cols = slice(0, width) if cols is None else cols
-            target = wide_tile((kind, s), [P, PACK, width], BF16, "wide_" + kind)
-            plane = source[s][:, t, cols].bitcast(FP8)
-            if on_vector:
-                nc.vector.tensor_scalar(out=target[:, t, cols], in0=plane, scalar1=scale, scalar2=None, op0=MULT)
+            if half is None:
+                target = wide_tile((kind, s), [P, PACK, source[s].shape[2]], BF16, "wide_" + kind)
+                plane = source[s][:, t, :].bitcast(FP8)
             else:
-                nc.scalar.activation(out=target[:, t, cols], in_=plane, func=COPY, scale=scale)
+                target = wide_tile((kind, s, half), [P, PACK, W], BF16, "wide_" + kind)
+                plane = source[s][:, t, half * W : (half + 1) * W].bitcast(FP8)
+            if on_vector:
+                nc.vector.tensor_scalar(out=target[:, t, :], in0=plane, scalar1=scale, scalar2=None, op0=MULT)
+            else:
+                nc.scalar.activation(out=target[:, t, :], in_=plane, func=COPY, scale=scale)
 
-        def group_tile(key, slots, names):
-            tag = "grouped%d" % slots
-            tile = stage.tile([P, slots * W * PACK], BF16, name=tag, tag=tag, align_bytes=64, bufs=5 - slots)
+        def group_tile(key, slots, names, own=False):
+            tag = "grouped_" + key if own else "grouped%d" % slots
+            tile = stage.tile([P, slots * W * PACK], BF16, name=tag, tag=tag, align_bytes=64, bufs=1 if own else 3)
             grouped[key] = (tile, names)
             for n, name in enumerate(names):
                 grouped[name] = tile[:, n * W * PACK : (n + 1) * W * PACK]
 
         def interleave(name, planes, permute=False, on_scalar=False):
-            if permute:
+            if on_scalar:
+                dst = grouped[name].rearrange("p (c j) -> p c j", j=PACK)
+                src = planes.rearrange("p j c -> p c j")
+            elif permute:
                 dst = grouped[name].rearrange("p (t m i j) -> p m j i t", t=PACK, i=2, j=PACK)
                 src = planes.rearrange("p j (m i t) -> p m j i t", i=2, t=PACK)
             else:
@@ -123,15 +136,14 @@ def tile_cross_layer_gram_sketch_d5_kernel(tc, F_bytes, F_scale, H_bytes, H_scal
         woven = {}
 
         def weave(s):
-            src = wide["h", s][:, :, 0:W].rearrange("p j c -> p c j")
+            src = wide["h", s][:, :, W:C2].rearrange("p j c -> p c j")
             for b in range(2):
                 woven[b] = bank(WEAVE_BANKS[b], [P, 2, W], "woven", BF16)
                 for q in range(2):
                     nc.tensor.matmul(woven[b][:, q, :], lhsT=ident_bf[:], rhs=src[:, (2 * b + q) * P : (2 * b + q + 1) * P, :], start=True, stop=True)
 
-        def weave_out(s):
-            for b in range(2):
-                nc.scalar.copy(out=grouped["h%d_0" % s][:, b * 2 * W : (b + 1) * 2 * W], in_=woven[b][:].rearrange("p q c -> p (q c)"))
+        def weave_out(s, b):
+            nc.scalar.copy(out=grouped["h%d_1" % s][:, b * 2 * W : (b + 1) * 2 * W], in_=woven[b][:].rearrange("p q c -> p (q c)"))
 
         def quantize(key, part=None, transient=False):
             tile, names = grouped[key]
@@ -171,73 +183,81 @@ def tile_cross_layer_gram_sketch_d5_kernel(tc, F_bytes, F_scale, H_bytes, H_scal
                 for u in range(2):
                     nc.tensor.transpose(turned[name, first][:, j, u, :], words[:, u::2], ident[:])
 
-        def turn_out(name, first, count):
-            dst = grouped[name][:, first * W : (first + count) * W].bitcast(F32).rearrange("p (j r u) -> p j r u", j=count, u=2)
+        def turn_out(name, first, target):
+            dst = target.bitcast(F32).rearrange("p (j r u) -> p j r u", j=2, u=2)
             nc.scalar.copy(out=dst, in_=turned[name, first][:].rearrange("p j u r -> p j r u"))
 
         last = PASSES - 1
+
+        def both(k):
+            return (["f%d" % k] if k < PASSES else ["h%d_1" % last]) + (["h%d_1" % (k - 2)] if k >= 2 else [])
+
+        group_tile("b0", 2, both(0))
         for k in range(PASSES):
             first_plane = H_ON_VECTOR.get(k, 0)
             on_scalar = F_ON_SCALAR.get(k + 1, 0)
-            for t in range(first_plane, max(first_plane, 2)):
-                widen("h", k, t, False, slice(0, W) if k == last else None)
-            if k >= 1:
-                group_tile("a%d" % (k - 1), 1, ["h%d_0" % (k - 1)])
-                weave_out(k - 1)
-            if k == U_PERIOD:
-                group_tile("ug", 1, ["u"])
-                for pair in range(2):
-                    turn("u", u_rows, 2 * pair, 2, WEAVE_BANKS[pair])
+            group_tile("b%d" % (k + 1), 2, both(k + 1))
             if k < last:
-                for t in range(max(first_plane, 2), PACK):
+                for t in range(first_plane, PACK):
                     widen("h", k, t, False)
-                if k == U_PERIOD:
+                    if t == 1:
+                        for j in range(on_scalar):
+                            widen("f", k + 1, j, False)
+                    if k - 1 in WOVEN and t >= 2:
+                        weave_out(k - 1, t - 2)
+                if k == U_PERIOD + 1:
+                    group_tile("ug", 1, ["u"], own=True)
                     for pair in range(2):
-                        turn_out("u", 2 * pair, 2)
-                for t in range(on_scalar):
-                    widen("f", k + 1, t, False)
+                        turn_out("u", 2 * pair, grouped["u"][:, pair * 2 * W : (pair + 1) * 2 * W])
             else:
-                for t in range(2, PACK):
-                    widen("h", k, t, False, slice(0, W))
                 for t in range(PACK):
-                    widen("h", k, t, False, slice(W, C2))
+                    widen("h", k, t, False, 0)
+                for t in range(PACK):
+                    widen("h", k, t, False, 1)
+                    if k - 1 in WOVEN and t < 2:
+                        weave_out(k - 1, t)
             if k == 0:
                 for t in range(PACK):
                     widen("f", 0, t, True)
                 for t in range(first_plane):
                     widen("h", 0, t, True)
-            if k < last:
+            if k in WOVEN:
                 weave(k)
-            else:
-                for t in range(2, PACK):
-                    for s in range(last - 1):
-                        gram_pass(s, 1, t)
-            names = ["f%d" % k] + (["h%d_1" % (k - 1)] if k >= 1 else [])
-            group_tile("b%d" % k, 2, names)
+            if k == U_PERIOD:
+                for pair in range(2):
+                    turn("u", u_rows, 2 * pair, 2, PACK + pair)
+            if k == last:
+                for s in range(last - 2):
+                    gram_pass(s, 1, 2)
             interleave("f%d" % k, wide["f", k][:], permute=True)
             if k >= 1:
-                interleave("h%d_1" % (k - 1), wide["h", k - 1][:, :, W:C2])
+                group_tile("a%d" % (k - 1), 1, ["h%d_0" % (k - 1)])
+                interleave("h%d_0" % (k - 1), wide["h", k - 1][:, :, 0:W])
+                if k - 1 not in WOVEN:
+                    interleave("h%d_1" % (k - 1), wide["h", k - 1][:, :, W:C2])
             if k < last:
                 for t in range(on_scalar, PACK):
                     widen("f", k + 1, t, True)
-            if k == U_PERIOD + 1:
+            if k == V_PERIOD:
+                group_tile("v", 2, ["v0", "v1"], own=True)
+                interleave("v0", v_rows[:, 0])
+            if k == U_PERIOD + 2:
                 quantize("ug")
-                nc.vector.tensor_copy(out=e_col[:], in_=e_bf[:])
-            if k in V_PERIODS:
-                if k == V_PERIODS[0]:
-                    group_tile("v", 2, ["v0", "v1"])
-                interleave("v%d" % V_PERIODS.index(k), v_rows[:, V_PERIODS.index(k)])
+            quantize("b%d" % k)
             if k >= 1:
                 quantize("a%d" % (k - 1), transient=True)
-            quantize("b%d" % k)
             if k >= 1:
                 for t in range(PACK):
                     gram_pass(k - 1, 0, t)
-                for t in range(PACK if k == last else 2):
-                    gram_pass(k - 1, 1, t)
+            if 2 <= k < last:
+                for t in range(2):
+                    gram_pass(k - 2, 1, t)
+
+            if k + RAW_BUFS < PASSES:
+                load_pass(k + RAW_BUFS, whole)
 
         d, de = {}, {}
-        dg = wide_tile("dg", [P, PACK, C2], BF16, "wide_h")
+        dg = {}
 
         def make_d(half, t):
             d[half] = wide_tile(("d", half), [P, PACK, W], F32, "wide_h")
@@ -249,10 +269,16 @@ def tile_cross_layer_gram_sketch_d5_kernel(tc, F_bytes, F_scale, H_bytes, H_scal
             de[half] = wide_tile(("de", half), [P, PACK, W], BF16, "wide_f")
             nc.scalar.activation(out=de[half][:, t, :], in_=d[half][:, t, :], func=COPY, scale=e_col[:, t : t + 1])
 
-        def make_dg(half, first, count):
-            cols = slice(half * W, (half + 1) * W)
-            ts = slice(first, first + count)
-            nc.vector.tensor_tensor(out=dg[:, ts, cols], in0=d[half][:, ts, :], in1=g_spread[:, cols].unsqueeze(1).to_broadcast([P, count, W]), op=MULT)
+        def make_dg(half, pair):
+            dg[half, pair] = stage.tile([P, 2, W], BF16, name="dg", bufs=4)
+            gains = g_spread[:, half * W : (half + 1) * W].unsqueeze(1).to_broadcast([P, 2, W])
+            nc.vector.tensor_tensor(out=dg[half, pair][:], in0=d[half][:, 2 * pair : 2 * pair + 2, :], in1=gains, op=MULT)
+
+        def turn_dg(half, pair, b):
+            turn(("dg", half, pair), dg[half, pair], 0, 2, b)
+
+        def turn_dg_out(half, pair):
+            turn_out(("dg", half, pair), 0, grouped["dg%d" % pair][:, half * 2 * W : (half + 1) * 2 * W])
 
         Y_rows = out_0.rearrange("(p t) r -> p t r", t=PACK)
         Z_rows = out_1.rearrange("(p t) c -> p t c", t=PACK)
@@ -265,7 +291,7 @@ def tile_cross_layer_gram_sketch_d5_kernel(tc, F_bytes, F_scale, H_bytes, H_scal
         def y_matmul(t, half, b):
             if half == 0:
                 acc["y", 0, t] = bank(b, [P, R], "y_acc")
-            matmul(acc["y", 0, t][:], "dg%d" % half, t, "v%d" % half, half == 0, half == HALVES - 1)
+            matmul(acc["y", 0, t][:], "dg%d" % (t // 2), 2 * half + t % 2, "v%d" % half, half == 0, half == HALVES - 1)
 
         def store(which, half, t, on_vector):
             result = stage.tile([P, W], F32, name="result", bufs=8)
@@ -277,64 +303,72 @@ def tile_cross_layer_gram_sketch_d5_kernel(tc, F_bytes, F_scale, H_bytes, H_scal
             nc.sync.dma_start(out=rows[:, t, half * W : (half + 1) * W], in_=result[:])
 
         ha, hb = "h%d_0" % last, "h%d_1" % last
+        interleave("v1", v_rows[:, 1], on_scalar=True)
         group_tile("a_last", 1, [ha])
-        interleave(ha, wide["h", last][:, :, 0:W])
+        interleave(ha, wide["h", last, 0][:])
         quantize("v", (0, W))
+        nc.vector.tensor_copy(out=e_col[:], in_=e_bf[:])
         quantize("a_last", transient=True)
         for t in range(PACK):
             gram_pass(last, 0, t)
-        group_tile("b_last", 1, [hb])
-        interleave(hb, wide["h", last][:, :, W:C2], on_scalar=True)
-        quantize("v", (W, 2 * W))
+        for s in range(last - 2):
+            gram_pass(s, 1, 3)
+        for t in range(PACK):
+            gram_pass(last - 2, 1, t)
+        interleave(hb, wide["h", last, 1][:])
         for t in range(PACK):
             make_d(0, t)
             make_de(0, t)
-            if t == 1:
-                quantize("b_last", transient=True)
+            if t == 0:
+                quantize("b%d" % PASSES)
                 for tt in range(PACK):
-                    gram_pass(last, 1, tt)
+                    for s in (last - 1, last):
+                        gram_pass(s, 1, tt)
         group_tile("de0g", 1, ["de0"])
         interleave("de0", de[0][:], on_scalar=True)
         for t in range(PACK):
             make_d(1, t)
             make_de(1, t)
         group_tile("dgg", 2, ["dg0", "dg1"])
-        make_dg(0, 0, 2)
-        turn("dg0", dg[:, :, 0:W], 0, 2, 0)
+        make_dg(0, 0)
+        turn_dg(0, 0, 4)
+        quantize("v", (W, 2 * W))
         quantize("de0g")
-        for t in range(3):
-            z_matmul(0, t, 1 + t)
-        make_dg(0, 2, 2)
-        turn("dg0", dg[:, :, 0:W], 2, 2, 4)
-        turn_out("dg0", 0, 2)
-        z_matmul(0, 3, 0)
+        for t in range(PACK):
+            z_matmul(0, t, t)
+        make_dg(1, 0)
+        turn_dg(1, 0, 5)
         group_tile("de1g", 1, ["de1"])
         interleave("de1", de[1][:])
-        store("z", 0, 0, False)
-        turn_out("dg0", 2, 2)
-        for t in range(1, PACK):
+        for t in range(PACK):
             store("z", 0, t, False)
-        make_dg(1, 0, 2)
-        turn("dg1", dg[:, :, W:C2], 0, 2, 1)
+            if t == TO_AT:
+                turn_dg_out(0, 0)
+        turn_dg_out(1, 0)
+        make_dg(0, 1)
+        turn_dg(0, 1, 6)
         quantize("de1g")
         for t in range(PACK):
-            z_matmul(1, t, PACK + (1 + t) % PACK)
-        turn_out("dg1", 0, 2)
-        make_dg(1, 2, 2)
-        turn("dg1", dg[:, :, W:C2], 2, 2, 2)
+            z_matmul(1, t, (7, 0, 1, 2)[t])
+        make_dg(1, 1)
+        turn_dg(1, 1, 3)
         quantize("dgg", (0, W))
+        for t in range(2):
+            y_matmul(t, 0, 4 + t)
+            y_matmul(t, 1, None)
+        turn_dg_out(0, 1)
         store("z", 1, 0, False)
         store("z", 1, 1, False)
+        turn_dg_out(1, 1)
         quantize("dgg", (W, W + 2 * P))
-        for t in range(2):
-            y_matmul(t, 0, t)
-            y_matmul(t, 1, t)
-        turn_out("dg1", 2, 2)
+        y_matmul(2, 0, 6)
+        y_matmul(3, 0, 7)
         store("z", 1, 2, True)
         quantize("dgg", (W + 2 * P, 2 * W))
-        for t in range(2, PACK):
-            y_matmul(t, 0, t)
-            y_matmul(t, 1, t)
+        y_matmul(2, 1, None)
+        y_matmul(3, 1, None)
         store("z", 1, 3, False)
-        for t in range(PACK):
-            store("y", 0, t, t % 2 == 0)
+        store("y", 0, 0, True)
+        store("y", 0, 1, False)
+        store("y", 0, 2, True)
+        store("y", 0, 3, False)

@@ -13,6 +13,7 @@ U8 = mybir.dt.uint8
 FP8 = mybir.dt.float8_e4m3fn
 FP8X4 = mybir.dt.float8_e4m3fn_x4
 MULT = mybir.AluOpType.mult
+ADD = mybir.AluOpType.add
 SUBTRACT = mybir.AluOpType.subtract
 COPY = mybir.ActivationFunctionType.Copy
 
@@ -20,17 +21,16 @@ P = 128
 PACK = 4
 W = 512
 PASSES = PIXELS // W
+LAST = PASSES - 1
 HALVES = C2 // W
 
-F_ON_SCALAR = {2: 1, 4: 1, 6: 1}
-H_ON_VECTOR = {0: 2}
-RAW_BUFS = 5
-WIDE_BUFS = {"wide_h": 3, "wide_f": 3}
-U_PERIOD = 1
-V_PERIOD = 5
-TO_AT = 3
+WOVEN = 6
 WEAVE_BANKS = (6, 7)
-WOVEN = list(range(PASSES - 1))
+U_BANKS = (4, 5)
+U_PERIOD = 1
+H_PLANES_ON_VECTOR = 2
+BYTE_BUFS = 5
+RESULT_BUFS = 8
 
 
 def tile_cross_layer_gram_sketch_d5_kernel(tc, F_bytes, F_scale, H_bytes, H_scale, A, g, e, V, U, out_0, out_1):
@@ -44,33 +44,33 @@ def tile_cross_layer_gram_sketch_d5_kernel(tc, F_bytes, F_scale, H_bytes, H_scal
         def bank(b, shape, name, dtype=F32):
             return psum.tile(shape, dtype, name=name, tag="bank%d" % b)
 
-        scale_rows = {"f": F_scale.rearrange("(s p t) o -> p s (t o)", p=P, t=PACK), "h": H_scale.rearrange("(s p t) o -> p s (t o)", p=P, t=PACK)}
+        scale_rows = {
+            "f": F_scale.rearrange("(s p t) o -> p s (t o)", p=P, t=PACK),
+            "h": H_scale.rearrange("(s p t) o -> p s (t o)", p=P, t=PACK),
+        }
         scale_first = {kind: keep.tile([P, 1, PACK], F32, name=kind + "_scale_first") for kind in "hf"}
-        scale_rest = {kind: keep.tile([P, PASSES - 1, PACK], F32, name=kind + "_scale_rest") for kind in "hf"}
+        scale_rest = {kind: keep.tile([P, LAST, PACK], F32, name=kind + "_scale_rest") for kind in "hf"}
         for kind in "hf":
             nc.scalar.dma_start(out=scale_first[kind][:], in_=scale_rows[kind][:, 0:1, :])
         for kind in "hf":
             nc.scalar.dma_start(out=scale_rest[kind][:], in_=scale_rows[kind][:, 1:PASSES, :])
-        warm_in = keep.tile([P, 1], F32, name="warm_in")
-        warm_out = keep.tile([P, 1], F32, name="warm_out")
-        nc.vector.memset(warm_in[:], 0.0)
-        nc.scalar.activation(out=warm_out[:], in_=warm_in[:], func=COPY)
 
         ident = keep.tile([P, P], F32, name="ident")
         make_identity(nc, ident[:])
         ident_bf = keep.tile([P, P], BF16, name="ident_bf")
-        make_identity(nc, ident_bf[:])
+        nc.scalar.activation(out=ident_bf[:], in_=ident[:], func=COPY)
 
-        F_rows = F_bytes.rearrange("(s p t) c -> s p t c", p=P, t=PACK)
-        H_rows = H_bytes.rearrange("(s p t) c -> s p t c", p=P, t=PACK)
-        f_bytes, h_bytes = {}, {}
+        byte_rows = {
+            "f": F_bytes.rearrange("(s p t) c -> s p t c", p=P, t=PACK),
+            "h": H_bytes.rearrange("(s p t) c -> s p t c", p=P, t=PACK),
+        }
+        raw = {}
 
         def load_pass(s, pieces):
-            f_bytes[s] = stage.tile([P, PACK, C1], U8, name="f_bytes", bufs=RAW_BUFS)
-            h_bytes[s] = stage.tile([P, PACK, C2], U8, name="h_bytes", bufs=RAW_BUFS)
+            raw["f", s] = stage.tile([P, PACK, C1], U8, name="f_bytes", bufs=BYTE_BUFS)
+            raw["h", s] = stage.tile([P, PACK, C2], U8, name="h_bytes", bufs=BYTE_BUFS)
             for kind, lo, hi in pieces:
-                target, rows = (f_bytes, F_rows) if kind == "f" else (h_bytes, H_rows)
-                nc.sync.dma_start(out=target[s][:, lo:hi, :], in_=rows[s][:, lo:hi, :])
+                nc.sync.dma_start(out=raw[kind, s][:, lo:hi, :], in_=byte_rows[kind][s][:, lo:hi, :])
 
         u_rows = keep.tile([P, PACK, C1], BF16, name="u_rows")
         v_rows = keep.tile([P, HALVES, PACK, R], BF16, name="v_rows")
@@ -81,294 +81,319 @@ def tile_cross_layer_gram_sketch_d5_kernel(tc, F_bytes, F_scale, H_bytes, H_scal
 
         whole = [("h", 0, PACK), ("f", 0, PACK)]
         load_pass(0, [("h", 2, 3), ("f", 0, 2), ("h", 3, 4), ("f", 2, 4), ("h", 0, 2)])
-        for s in range(1, RAW_BUFS):
+        for s in range(1, BYTE_BUFS):
             load_pass(s, whole)
-            if s == 2:
+            if s == U_PERIOD + 1:
                 nc.sync.dma_start(out=u_rows[:], in_=U.rearrange("(p t) c -> p t c", t=PACK))
         nc.sync.dma_start(out=v_rows[:], in_=V.rearrange("(h p t) r -> p h t r", p=P, t=PACK))
         nc.sync.dma_start(out=a_rows[:], in_=A.rearrange("(p t) c -> p t c", t=PACK))
         nc.sync.dma_start(out=e_bf[:], in_=e.rearrange("(p t) -> p t", t=PACK))
         nc.sync.dma_start(out=g_spread[:], in_=g.partition_broadcast(P))
 
-        wide, grouped, mx = {}, {}, {}
+        planes = {}
+        grouped = {}
+        batch = {}
+        mx = {}
 
-        def wide_tile(key, shape, dtype, tag):
-            if key not in wide:
-                wide[key] = stage.tile(shape, dtype, name=tag, tag=tag, bufs=WIDE_BUFS[tag])
-            return wide[key]
+        def plane_tile(key, columns, dtype, tag):
+            if key not in planes:
+                planes[key] = stage.tile([P, PACK, columns], dtype, name=tag, tag=tag)
+            return planes[key]
 
-        def widen(kind, s, t, on_vector, half=None):
-            source = f_bytes if kind == "f" else h_bytes
+        def widen(kind, s, t, on_vector=False, half=None):
             scale = scale_first[kind][:, 0, t : t + 1] if s == 0 else scale_rest[kind][:, s - 1, t : t + 1]
             if half is None:
-                target = wide_tile((kind, s), [P, PACK, source[s].shape[2]], BF16, "wide_" + kind)
-                plane = source[s][:, t, :].bitcast(FP8)
+                target = plane_tile((kind, s), raw[kind, s].shape[2], BF16, "wide_" + kind)
+                source = raw[kind, s][:, t, :].bitcast(FP8)
             else:
-                target = wide_tile((kind, s, half), [P, PACK, W], BF16, "wide_" + kind)
-                plane = source[s][:, t, half * W : (half + 1) * W].bitcast(FP8)
+                target = plane_tile((kind, s, half), W, BF16, "wide_" + kind)
+                source = raw[kind, s][:, t, half * W : (half + 1) * W].bitcast(FP8)
             if on_vector:
-                nc.vector.tensor_scalar(out=target[:, t, :], in0=plane, scalar1=scale, scalar2=None, op0=MULT)
+                nc.vector.tensor_scalar(out=target[:, t, :], in0=source, scalar1=scale, scalar2=None, op0=MULT)
             else:
-                nc.scalar.activation(out=target[:, t, :], in_=plane, func=COPY, scale=scale)
+                nc.scalar.activation(out=target[:, t, :], in_=source, func=COPY, scale=scale)
 
-        def group_tile(key, slots, names, own=False):
-            tag = "grouped_" + key if own else "grouped%d" % slots
-            tile = stage.tile([P, slots * W * PACK], BF16, name=tag, tag=tag, align_bytes=64, bufs=1 if own else 3)
-            grouped[key] = (tile, names)
+        def new_batch(key, names, slots=1, own_tag=None):
+            tag = own_tag or "grouped%d" % slots
+            tile = stage.tile([P, slots * W * PACK], BF16, name=tag, tag=tag, align_bytes=64, bufs=1 if own_tag else 3)
+            batch[key] = (tile, names)
             for n, name in enumerate(names):
                 grouped[name] = tile[:, n * W * PACK : (n + 1) * W * PACK]
 
-        def interleave(name, planes, permute=False, on_scalar=False):
-            if on_scalar:
-                dst = grouped[name].rearrange("p (c j) -> p c j", j=PACK)
-                src = planes.rearrange("p j c -> p c j")
-            elif permute:
-                dst = grouped[name].rearrange("p (t m i j) -> p m j i t", t=PACK, i=2, j=PACK)
-                src = planes.rearrange("p j (m i t) -> p m j i t", i=2, t=PACK)
-            else:
-                dst = grouped[name].rearrange("p (c i j) -> p c j i", i=4, j=PACK)
-                src = planes.rearrange("p j (c i) -> p c j i", i=4)
-            if on_scalar:
-                nc.scalar.copy(out=dst, in_=src)
-            else:
-                nc.vector.tensor_copy(out=dst, in_=src)
+        def interleave_vector(target, source):
+            nc.vector.tensor_copy(
+                out=target.rearrange("p (c i t) -> p c t i", i=4, t=PACK),
+                in_=source.rearrange("p t (c i) -> p c t i", i=4),
+            )
+
+        def interleave_f(s):
+            nc.vector.tensor_copy(
+                out=grouped["f%d" % s].rearrange("p (j n i t) -> p n t i j", j=PACK, i=2, t=PACK),
+                in_=planes["f", s][:].rearrange("p t (n i j) -> p n t i j", i=2, j=PACK),
+            )
+
+        def interleave_scalar(target, source):
+            nc.scalar.copy(out=target.rearrange("p (c t) -> p c t", t=PACK), in_=source.rearrange("p t c -> p c t"))
+
+        def column_half(name, source, n):
+            return grouped[name][:, n * 2 * W : (n + 1) * 2 * W], source[:, :, n * W // 2 : (n + 1) * W // 2]
 
         woven = {}
 
-        def weave(s):
-            src = wide["h", s][:, :, W:C2].rearrange("p j c -> p c j")
-            for b in range(2):
-                woven[b] = bank(WEAVE_BANKS[b], [P, 2, W], "woven", BF16)
+        def weave(source, banks):
+            columns = source.rearrange("p t c -> p c t")
+            for n in range(2):
+                woven[n] = bank(banks[n], [P, 2, W], "woven", BF16)
                 for q in range(2):
-                    nc.tensor.matmul(woven[b][:, q, :], lhsT=ident_bf[:], rhs=src[:, (2 * b + q) * P : (2 * b + q + 1) * P, :], start=True, stop=True)
+                    first = (2 * n + q) * P
+                    nc.tensor.matmul(woven[n][:, q, :], lhsT=ident_bf[:], rhs=columns[:, first : first + P, :], start=True, stop=True)
 
-        def weave_out(s, b):
-            nc.scalar.copy(out=grouped["h%d_1" % s][:, b * 2 * W : (b + 1) * 2 * W], in_=woven[b][:].rearrange("p q c -> p (q c)"))
+        def weave_out(name, n):
+            nc.scalar.copy(out=grouped[name][:, n * 2 * W : (n + 1) * 2 * W], in_=woven[n][:].rearrange("p q c -> p (q c)"))
 
-        def quantize(key, part=None, transient=False):
-            tile, names = grouped[key]
+        def quantize(key, cols=None, rotating=False):
+            tile, names = batch[key]
             columns = len(names) * W
             if key not in mx:
-                if transient:
-                    mx[key] = (stage.tile([P, columns], U32, name="h_codes", align_bytes=64),
-                               stage.tile([P, columns], U8, name="h_scales", align_bytes=64))
-                else:
-                    mx[key] = (keep.tile([P, columns], U32, name="codes_" + key, align_bytes=64),
-                               keep.tile([P, columns], U8, name="scales_" + key, align_bytes=64))
+                pool, suffix = (stage, "rotating") if rotating else (keep, key)
+                codes = pool.tile([P, columns], U32, name="codes_" + suffix, align_bytes=64)
+                scales = pool.tile([P, columns], U8, name="scales_" + suffix, align_bytes=64)
+                mx[key] = (codes, scales)
                 for n, name in enumerate(names):
-                    mx[name] = (mx[key][0][:, n * W : (n + 1) * W], mx[key][1][:, n * W : (n + 1) * W])
+                    mx[name] = (codes[:, n * W : (n + 1) * W], scales[:, n * W : (n + 1) * W])
             codes, scales = mx[key]
-            lo, hi = (0, columns) if part is None else part
+            lo, hi = cols or (0, columns)
             nc.vector.quantize_mx(out=codes[:, lo:hi].bitcast(FP8X4), scales=scales[:, lo:hi], in_=tile[:, lo * PACK : hi * PACK])
 
-        def matmul(out, left, t, right, start, stop):
-            rows = slice(t * P, (t + 1) * P)
+        def mx_pass(out, left, block, right, start, stop):
+            cols = slice(block * P, (block + 1) * P)
             nc.tensor.matmul_mx(
-                out=out, lhsT=mx[left][0][:, rows].bitcast(FP8X4), lhsT_scale=mx[left][1][:, rows],
-                rhs=mx[right][0].bitcast(FP8X4), rhs_scale=mx[right][1], start=start, stop=stop)
+                out=out,
+                lhsT=mx[left][0][:, cols].bitcast(FP8X4),
+                lhsT_scale=mx[left][1][:, cols],
+                rhs=mx[right][0].bitcast(FP8X4),
+                rhs_scale=mx[right][1],
+                start=start,
+                stop=stop,
+            )
 
         gram = {}
 
         def gram_pass(s, half, t):
             if s == 0:
                 gram[half, t] = bank(PACK * half + t, [P, W], "gram")
-            matmul(gram[half, t][:], "f%d" % s, t, "h%d_%d" % (s, half), s == 0, s == PASSES - 1)
+            mx_pass(gram[half, t][:], "f%d" % s, t, "h%d_%d" % (s, half), s == 0, s == LAST)
 
         turned = {}
 
-        def turn(name, rows, first, count, b):
-            turned[name, first] = bank(b, [P, count, 2, P], "turned")
-            for j in range(count):
-                words = rows[:, first + j, :].bitcast(F32)
+        def turn(key, rows, b):
+            turned[key] = bank(b, [P, 2, 2, P], "turned")
+            for j in range(2):
+                words = rows[:, j, :].bitcast(F32)
                 for u in range(2):
-                    nc.tensor.transpose(turned[name, first][:, j, u, :], words[:, u::2], ident[:])
+                    nc.tensor.transpose(turned[key][:, j, u, :], words[:, u::2], ident[:])
 
-        def turn_out(name, first, target):
-            dst = target.bitcast(F32).rearrange("p (j r u) -> p j r u", j=2, u=2)
-            nc.scalar.copy(out=dst, in_=turned[name, first][:].rearrange("p j u r -> p j r u"))
+        def turn_out(key, target):
+            nc.scalar.copy(
+                out=target.bitcast(F32).rearrange("p (j r u) -> p j r u", j=2, u=2),
+                in_=turned[key][:].rearrange("p j u r -> p j r u"),
+            )
 
-        last = PASSES - 1
+        def kept_names(k):
+            return ["f%d" % k if k < PASSES else "h%d_1" % LAST] + (["h%d_1" % (k - 2)] if k >= 2 else [])
 
-        def both(k):
-            return (["f%d" % k] if k < PASSES else ["h%d_1" % last]) + (["h%d_1" % (k - 2)] if k >= 2 else [])
-
-        group_tile("b0", 2, both(0))
+        new_batch("kept0", kept_names(0), slots=2)
         for k in range(PASSES):
-            first_plane = H_ON_VECTOR.get(k, 0)
-            on_scalar = F_ON_SCALAR.get(k + 1, 0)
-            group_tile("b%d" % (k + 1), 2, both(k + 1))
-            if k < last:
-                for t in range(first_plane, PACK):
-                    widen("h", k, t, False)
-                    if t == 1:
-                        for j in range(on_scalar):
-                            widen("f", k + 1, j, False)
-                    if k - 1 in WOVEN and t >= 2:
-                        weave_out(k - 1, t - 2)
-                if k == U_PERIOD + 1:
-                    group_tile("ug", 1, ["u"], own=True)
-                    for pair in range(2):
-                        turn_out("u", 2 * pair, grouped["u"][:, pair * 2 * W : (pair + 1) * 2 * W])
+            new_batch("kept%d" % (k + 1), kept_names(k + 1), slots=2, own_tag="grouped_late" if k == LAST else None)
+            if k < LAST:
+                for t in range(H_PLANES_ON_VECTOR if k == 0 else 0, PACK):
+                    widen("h", k, t)
+                    if 1 <= k <= WOVEN and t >= 2:
+                        weave_out("h%d_1" % (k - 1), t - 2)
             else:
-                for t in range(PACK):
-                    widen("h", k, t, False, 0)
-                for t in range(PACK):
-                    widen("h", k, t, False, 1)
-                    if k - 1 in WOVEN and t < 2:
-                        weave_out(k - 1, t)
+                for half in range(HALVES):
+                    for t in range(PACK):
+                        widen("h", k, t, half=half)
+            if k == U_PERIOD + 1:
+                new_batch("u_batch", ["u"], own_tag="grouped_weights")
+                for pair in range(2):
+                    turn_out(("u", pair), grouped["u"][:, pair * 2 * W : (pair + 1) * 2 * W])
             if k == 0:
                 for t in range(PACK):
-                    widen("f", 0, t, True)
-                for t in range(first_plane):
-                    widen("h", 0, t, True)
-            if k in WOVEN:
-                weave(k)
+                    widen("f", 0, t, on_vector=True)
+                for t in range(H_PLANES_ON_VECTOR):
+                    widen("h", 0, t, on_vector=True)
+            if k < WOVEN:
+                weave(planes["h", k][:, :, W:C2], WEAVE_BANKS)
             if k == U_PERIOD:
                 for pair in range(2):
-                    turn("u", u_rows, 2 * pair, 2, PACK + pair)
-            if k == last:
-                for s in range(last - 2):
-                    gram_pass(s, 1, 2)
-            interleave("f%d" % k, wide["f", k][:], permute=True)
+                    turn(("u", pair), u_rows[:, 2 * pair : 2 * pair + 2, :], U_BANKS[pair])
+            if k == LAST:
+                for t in range(2, PACK):
+                    for s in range(k - 2):
+                        gram_pass(s, 1, t)
+            interleave_f(k)
             if k >= 1:
-                group_tile("a%d" % (k - 1), 1, ["h%d_0" % (k - 1)])
-                interleave("h%d_0" % (k - 1), wide["h", k - 1][:, :, 0:W])
-                if k - 1 not in WOVEN:
-                    interleave("h%d_1" % (k - 1), wide["h", k - 1][:, :, W:C2])
-            if k < last:
-                for t in range(on_scalar, PACK):
-                    widen("f", k + 1, t, True)
-            if k == V_PERIOD:
-                group_tile("v", 2, ["v0", "v1"], own=True)
-                interleave("v0", v_rows[:, 0])
+                new_batch("first%d" % (k - 1), ["h%d_0" % (k - 1)])
+                interleave_vector(grouped["h%d_0" % (k - 1)], planes["h", k - 1][:, :, 0:W])
+                if k > WOVEN:
+                    interleave_vector(grouped["h%d_1" % (k - 1)], planes["h", k - 1][:, :, W:C2])
+            if k < LAST:
+                for t in range(PACK):
+                    widen("f", k + 1, t, on_vector=True)
             if k == U_PERIOD + 2:
-                quantize("ug")
-            quantize("b%d" % k)
+                quantize("u_batch")
+            quantize("kept%d" % k)
             if k >= 1:
-                quantize("a%d" % (k - 1), transient=True)
-            if k >= 1:
+                quantize("first%d" % (k - 1), rotating=True)
                 for t in range(PACK):
                     gram_pass(k - 1, 0, t)
-            if 2 <= k < last:
+            if 2 <= k < LAST:
                 for t in range(2):
                     gram_pass(k - 2, 1, t)
+            if k + BYTE_BUFS < PASSES:
+                load_pass(k + BYTE_BUFS, whole)
 
-            if k + RAW_BUFS < PASSES:
-                load_pass(k + RAW_BUFS, whole)
+        free_banks = []
+        held = {}
 
-        d, de = {}, {}
-        dg = {}
+        def take(key):
+            held[key] = free_banks.pop(0)
+            return held[key]
+
+        def release(key):
+            free_banks.append(held[key])
 
         def make_d(half, t):
-            d[half] = wide_tile(("d", half), [P, PACK, W], F32, "wide_h")
+            d = plane_tile(("d", half), W, F32, "wide_h")
             nc.vector.scalar_tensor_tensor(
-                out=d[half][:, t, :], in0=gram[half, t][:], scalar=1.0 / PIXELS,
-                in1=a_rows[:, t, half * W : (half + 1) * W], op0=MULT, op1=SUBTRACT)
+                out=d[:, t, :], in0=gram[half, t][:], scalar=1.0 / PIXELS,
+                in1=a_rows[:, t, half * W : (half + 1) * W], op0=MULT, op1=SUBTRACT,
+            )
+            free_banks.append(PACK * half + t)
 
         def make_de(half, t):
-            de[half] = wide_tile(("de", half), [P, PACK, W], BF16, "wide_f")
-            nc.scalar.activation(out=de[half][:, t, :], in_=d[half][:, t, :], func=COPY, scale=e_col[:, t : t + 1])
+            de = plane_tile(("de", half), W, BF16, "wide_f")
+            nc.scalar.activation(out=de[:, t, :], in_=planes["d", half][:, t, :], func=COPY, scale=e_col[:, t : t + 1])
+
+        dg = {}
 
         def make_dg(half, pair):
-            dg[half, pair] = stage.tile([P, 2, W], BF16, name="dg", bufs=4)
+            dg[half, pair] = stage.tile([P, 2, W], BF16, name="dg", bufs=HALVES * 2)
             gains = g_spread[:, half * W : (half + 1) * W].unsqueeze(1).to_broadcast([P, 2, W])
-            nc.vector.tensor_tensor(out=dg[half, pair][:], in0=d[half][:, 2 * pair : 2 * pair + 2, :], in1=gains, op=MULT)
+            nc.vector.tensor_tensor(out=dg[half, pair][:], in0=planes["d", half][:, 2 * pair : 2 * pair + 2, :], in1=gains, op=MULT)
 
-        def turn_dg(half, pair, b):
-            turn(("dg", half, pair), dg[half, pair], 0, 2, b)
+        def turn_dg(half, pair):
+            turn(("dg", half, pair), dg[half, pair], take(("dg", half, pair)))
 
         def turn_dg_out(half, pair):
-            turn_out(("dg", half, pair), 0, grouped["dg%d" % pair][:, half * 2 * W : (half + 1) * 2 * W])
+            turn_out(("dg", half, pair), grouped["dg%d" % pair][:, half * 2 * W : (half + 1) * 2 * W])
+            release(("dg", half, pair))
 
-        Y_rows = out_0.rearrange("(p t) r -> p t r", t=PACK)
-        Z_rows = out_1.rearrange("(p t) c -> p t c", t=PACK)
-        acc = {}
+        def quantize_dg(half, pair):
+            lo = pair * W + half * 2 * P
+            quantize("dg_batch", (lo, lo + 2 * P))
 
-        def z_matmul(half, t, b):
-            acc["z", half, t] = bank(b, [P, W], "z_acc")
-            matmul(acc["z", half, t][:], "u", t, "de%d" % half, True, True)
+        sums = {}
 
-        def y_matmul(t, half, b):
+        def z_pass(half, j):
+            sums["z", half, j] = bank(take(("z", half, j)), [P, W], "z_sum")
+            mx_pass(sums["z", half, j][:], "u", j, "de%d" % half, True, True)
+
+        def y_pass(t, half):
             if half == 0:
-                acc["y", 0, t] = bank(b, [P, R], "y_acc")
-            matmul(acc["y", 0, t][:], "dg%d" % (t // 2), 2 * half + t % 2, "v%d" % half, half == 0, half == HALVES - 1)
+                sums["y", 0, t] = bank(take(("y", 0, t)), [P, R], "y_sum")
+            mx_pass(sums["y", 0, t][:], "dg%d" % (t // 2), 2 * half + t % 2, "v%d" % half, half == 0, half == HALVES - 1)
 
-        def store(which, half, t, on_vector):
-            result = stage.tile([P, W], F32, name="result", bufs=8)
+        out_rows = {"y": out_0.rearrange("(p t) r -> p t r", t=PACK), "z": out_1.rearrange("(p t) c -> p t c", t=PACK)}
+
+        def store(which, half, t, on_vector=False):
+            result = stage.tile([P, W], F32, name="result", bufs=RESULT_BUFS)
             if on_vector:
-                nc.vector.tensor_copy(out=result[:], in_=acc[which, half, t][:])
+                nc.vector.tensor_copy(out=result[:], in_=sums[which, half, t][:])
             else:
-                nc.scalar.copy(out=result[:], in_=acc[which, half, t][:])
-            rows = Y_rows if which == "y" else Z_rows
-            nc.sync.dma_start(out=rows[:, t, half * W : (half + 1) * W], in_=result[:])
+                nc.scalar.copy(out=result[:], in_=sums[which, half, t][:])
+            nc.sync.dma_start(out=out_rows[which][:, t, half * W : (half + 1) * W], in_=result[:])
+            release((which, half, t))
 
-        ha, hb = "h%d_0" % last, "h%d_1" % last
-        interleave("v1", v_rows[:, 1], on_scalar=True)
-        group_tile("a_last", 1, [ha])
-        interleave(ha, wide["h", last, 0][:])
-        quantize("v", (0, W))
+        new_batch("v1_batch", ["v1"], own_tag="grouped_weights")
+        new_batch("first_last", ["h%d_0" % LAST])
+        new_batch("dg_batch", ["dg0", "dg1"], slots=2)
+        interleave_scalar(grouped["h%d_1" % LAST], planes["h", LAST, 1][:])
+        for n in range(2):
+            interleave_scalar(*column_half("v1", v_rows[:, 1], n))
+        interleave_vector(grouped["h%d_0" % LAST], planes["h", LAST, 0][:])
         nc.vector.tensor_copy(out=e_col[:], in_=e_bf[:])
-        quantize("a_last", transient=True)
+        quantize("first_last", rotating=True)
+        quantize("kept%d" % PASSES)
+
+        new_batch("v0_batch", ["v0"], own_tag="grouped_late")
+        nc.gpsimd.tensor_scalar(
+            out=grouped["v0"].rearrange("p (c t) -> p c t", t=PACK), in0=v_rows[:, 0].rearrange("p t c -> p c t"),
+            scalar1=1.0, scalar2=0.0, op0=MULT, op1=ADD,
+        )
         for t in range(PACK):
-            gram_pass(last, 0, t)
-        for s in range(last - 2):
-            gram_pass(s, 1, 3)
+            gram_pass(LAST, 0, t)
         for t in range(PACK):
-            gram_pass(last - 2, 1, t)
-        interleave(hb, wide["h", last, 1][:])
+            for s in range(LAST - 2, PASSES):
+                gram_pass(s, 1, t)
+
         for t in range(PACK):
             make_d(0, t)
             make_de(0, t)
-            if t == 0:
-                quantize("b%d" % PASSES)
-                for tt in range(PACK):
-                    for s in (last - 1, last):
-                        gram_pass(s, 1, tt)
-        group_tile("de0g", 1, ["de0"])
-        interleave("de0", de[0][:], on_scalar=True)
+        new_batch("de0_batch", ["de0"])
+        weave(planes["de", 0][:], [take(("woven", n)) for n in range(2)])
         for t in range(PACK):
             make_d(1, t)
+        for t in range(PACK):
             make_de(1, t)
-        group_tile("dgg", 2, ["dg0", "dg1"])
-        make_dg(0, 0)
-        turn_dg(0, 0, 4)
-        quantize("v", (W, 2 * W))
-        quantize("de0g")
-        for t in range(PACK):
-            z_matmul(0, t, t)
-        make_dg(1, 0)
-        turn_dg(1, 0, 5)
-        group_tile("de1g", 1, ["de1"])
-        interleave("de1", de[1][:])
-        for t in range(PACK):
-            store("z", 0, t, False)
-            if t == TO_AT:
-                turn_dg_out(0, 0)
-        turn_dg_out(1, 0)
+            if t >= 2:
+                weave_out("de0", t - 2)
+                release(("woven", t - 2))
+
+        for half in range(HALVES):
+            make_dg(half, 0)
+            turn_dg(half, 0)
+        quantize("de0_batch")
+        for j in range(PACK):
+            z_pass(0, j)
+        new_batch("de1_batch", ["de1"])
+        interleave_scalar(*column_half("de1", planes["de", 1][:], 0))
+        for half in range(HALVES):
+            turn_dg_out(half, 0)
+        for j in range(2):
+            store("z", 0, j)
+        interleave_vector(*column_half("de1", planes["de", 1][:], 1))
         make_dg(0, 1)
-        turn_dg(0, 1, 6)
-        quantize("de1g")
-        for t in range(PACK):
-            z_matmul(1, t, (7, 0, 1, 2)[t])
+        quantize("de1_batch")
+        for j in range(2):
+            z_pass(1, j)
+        for j in range(2, PACK):
+            store("z", 0, j)
+        for j in range(2, PACK):
+            z_pass(1, j)
+        quantize_dg(0, 0)
         make_dg(1, 1)
-        turn_dg(1, 1, 3)
-        quantize("dgg", (0, W))
-        for t in range(2):
-            y_matmul(t, 0, 4 + t)
-            y_matmul(t, 1, None)
+        for half in range(HALVES):
+            turn_dg(half, 1)
+        for j in range(2):
+            store("z", 1, j)
+        quantize("v0_batch")
+        quantize_dg(1, 0)
+        quantize("v1_batch")
         turn_dg_out(0, 1)
-        store("z", 1, 0, False)
-        store("z", 1, 1, False)
+        for t in range(2):
+            y_pass(t, 0)
+        store("z", 1, 2)
+        quantize_dg(0, 1)
+        for t in range(2):
+            y_pass(t, 1)
         turn_dg_out(1, 1)
-        quantize("dgg", (W, W + 2 * P))
-        y_matmul(2, 0, 6)
-        y_matmul(3, 0, 7)
-        store("z", 1, 2, True)
-        quantize("dgg", (W + 2 * P, 2 * W))
-        y_matmul(2, 1, None)
-        y_matmul(3, 1, None)
-        store("z", 1, 3, False)
-        store("y", 0, 0, True)
-        store("y", 0, 1, False)
-        store("y", 0, 2, True)
-        store("y", 0, 3, False)
+        store("z", 1, 3, on_vector=True)
+        for t in range(2, PACK):
+            y_pass(t, 0)
+        quantize_dg(1, 1)
+        for t in range(2, PACK):
+            y_pass(t, 1)
+        for t in range(PACK):
+            store("y", 0, t, on_vector=t in (1, 2))

@@ -29,6 +29,7 @@ WEAVE_BANKS = (6, 7)
 U_BANKS = (4, 5)
 U_PERIOD = 1
 H_PLANES_ON_VECTOR = 2
+EARLY = 2
 BYTE_BUFS = 5
 RESULT_BUFS = 8
 
@@ -48,12 +49,10 @@ def tile_cross_layer_gram_sketch_d5_kernel(tc, F_bytes, F_scale, H_bytes, H_scal
             "f": F_scale.rearrange("(s p t) o -> p s (t o)", p=P, t=PACK),
             "h": H_scale.rearrange("(s p t) o -> p s (t o)", p=P, t=PACK),
         }
-        scale_first = {kind: keep.tile([P, 1, PACK], F32, name=kind + "_scale_first") for kind in "hf"}
-        scale_rest = {kind: keep.tile([P, LAST, PACK], F32, name=kind + "_scale_rest") for kind in "hf"}
-        for kind in "hf":
-            nc.scalar.dma_start(out=scale_first[kind][:], in_=scale_rows[kind][:, 0:1, :])
-        for kind in "hf":
-            nc.scalar.dma_start(out=scale_rest[kind][:], in_=scale_rows[kind][:, 1:PASSES, :])
+        scale_first = {kind: keep.tile([P, EARLY, PACK], F32, name=kind + "_scale_first") for kind in "fh"}
+        scale_rest = {kind: keep.tile([P, PASSES - EARLY, PACK], F32, name=kind + "_scale_rest") for kind in "fh"}
+        for kind in "fh":
+            nc.scalar.dma_start(out=scale_first[kind][:], in_=scale_rows[kind][:, 0:EARLY, :])
 
         ident = keep.tile([P, P], F32, name="ident")
         make_identity(nc, ident[:])
@@ -80,9 +79,12 @@ def tile_cross_layer_gram_sketch_d5_kernel(tc, F_bytes, F_scale, H_bytes, H_scal
         g_spread = keep.tile([P, C2], BF16, name="g_spread")
 
         whole = [("h", 0, PACK), ("f", 0, PACK)]
-        load_pass(0, [("h", 2, 3), ("f", 0, 2), ("h", 3, 4), ("f", 2, 4), ("h", 0, 2)])
+        load_pass(0, [("f", 0, 2), ("h", 2, 3), ("f", 2, 4), ("h", 3, 4), ("h", 0, 2)])
         for s in range(1, BYTE_BUFS):
-            load_pass(s, whole)
+            load_pass(s, [("h", 0, 2), ("h", 2, 4), ("f", 0, PACK)] if s == 1 else whole)
+            if s == EARLY - 1:
+                for kind in "fh":
+                    nc.sync.dma_start(out=scale_rest[kind][:], in_=scale_rows[kind][:, EARLY:PASSES, :])
             if s == U_PERIOD + 1:
                 nc.sync.dma_start(out=u_rows[:], in_=U.rearrange("(p t) c -> p t c", t=PACK))
         nc.sync.dma_start(out=v_rows[:], in_=V.rearrange("(h p t) r -> p h t r", p=P, t=PACK))
@@ -101,7 +103,7 @@ def tile_cross_layer_gram_sketch_d5_kernel(tc, F_bytes, F_scale, H_bytes, H_scal
             return planes[key]
 
         def widen(kind, s, t, on_vector=False, half=None):
-            scale = scale_first[kind][:, 0, t : t + 1] if s == 0 else scale_rest[kind][:, s - 1, t : t + 1]
+            scale = scale_first[kind][:, s, t : t + 1] if s < EARLY else scale_rest[kind][:, s - EARLY, t : t + 1]
             if half is None:
                 target = plane_tile((kind, s), raw[kind, s].shape[2], BF16, "wide_" + kind)
                 source = raw[kind, s][:, t, :].bitcast(FP8)

from contextlib import ExitStack

import concourse.mybir as mybir
from concourse.masks import make_identity

PIXELS, C1, C2, R = 4096, 512, 1024, 512
FLOPS = 2 * PIXELS * C1 * C2 + 2 * C1 * C2 * R + 2 * R * C1 * C2

F32 = mybir.dt.float32
BF16 = mybir.dt.bfloat16
U32 = mybir.dt.uint32
U8 = mybir.dt.uint8
FP8 = mybir.dt.float8_e4m3fn
FP8X4 = mybir.dt.float8_e4m3fn_x4
MULT = mybir.AluOpType.mult
ADD = mybir.AluOpType.add
SUBTRACT = mybir.AluOpType.subtract
COPY = mybir.ActivationFunctionType.Copy

P = 128
PACK = 4
W = 512
PASSES = PIXELS // W
LAST = PASSES - 1
HALVES = C2 // W

WOVEN = 6
WEAVE_BANKS = (6, 7)
U_BANKS = (4, 5)
U_PERIOD = 1
H_PLANES_ON_VECTOR = 2
EARLY = 2
BYTE_BUFS = 5
RESULT_BUFS = 8


def tile_cross_layer_gram_sketch_d5_kernel(tc, F_bytes, F_scale, H_bytes, H_scale, A, g, e, V, U, out_0, out_1):
    nc = tc.nc
    with ExitStack() as ctx:
        keep = ctx.enter_context(tc.tile_pool(name="keep", bufs=1))
        stage = ctx.enter_context(tc.tile_pool(name="stage", bufs=3))
        psum = ctx.enter_context(tc.psum_pool(name="psum", bufs=1))
        ctx.enter_context(tc.manual_schedule())

        def bank(b, shape, name, dtype=F32):
            return psum.tile(shape, dtype, name=name, tag="bank%d" % b)

        scale_rows = {
            "f": F_scale.rearrange("(s p t) o -> p s (t o)", p=P, t=PACK),
            "h": H_scale.rearrange("(s p t) o -> p s (t o)", p=P, t=PACK),
        }
        scale_first = {kind: keep.tile([P, EARLY, PACK], F32, name=kind + "_scale_first") for kind in "fh"}
        scale_rest = {kind: keep.tile([P, PASSES - EARLY, PACK], F32, name=kind + "_scale_rest") for kind in "fh"}
        for kind in "fh":
            nc.scalar.dma_start(out=scale_first[kind][:], in_=scale_rows[kind][:, 0:EARLY, :])

        ident = keep.tile([P, P], F32, name="ident")
        make_identity(nc, ident[:])
        ident_bf = keep.tile([P, P], BF16, name="ident_bf")
        nc.scalar.activation(out=ident_bf[:], in_=ident[:], func=COPY)

        byte_rows = {
            "f": F_bytes.rearrange("(s p t) c -> s p t c", p=P, t=PACK),
            "h": H_bytes.rearrange("(s p t) c -> s p t c", p=P, t=PACK),
        }
        raw = {}

        def load_pass(s, pieces):
            raw["f", s] = stage.tile([P, PACK, C1], U8, name="f_bytes", bufs=BYTE_BUFS)
            raw["h", s] = stage.tile([P, PACK, C2], U8, name="h_bytes", bufs=BYTE_BUFS)
            for kind, lo, hi in pieces:
                nc.sync.dma_start(out=raw[kind, s][:, lo:hi, :], in_=byte_rows[kind][s][:, lo:hi, :])

        u_rows = keep.tile([P, PACK, C1], BF16, name="u_rows")
        v_rows = keep.tile([P, HALVES, PACK, R], BF16, name="v_rows")
        a_rows = keep.tile([P, PACK, C2], BF16, name="a_rows")
        e_bf = keep.tile([P, PACK], BF16, name="e_bf")
        e_col = keep.tile([P, PACK], F32, name="e_col")
        g_spread = keep.tile([P, C2], BF16, name="g_spread")

        whole = [("h", 0, PACK), ("f", 0, PACK)]
        load_pass(0, [("f", 0, 2), ("h", 2, 3), ("f", 2, 4), ("h", 3, 4), ("h", 0, 2)])
        for s in range(1, BYTE_BUFS):
            load_pass(s, [("h", 0, 2), ("h", 2, 4), ("f", 0, PACK)] if s == 1 else whole)
            if s == EARLY - 1:
                for kind in "fh":
                    nc.sync.dma_start(out=scale_rest[kind][:], in_=scale_rows[kind][:, EARLY:PASSES, :])
            if s == U_PERIOD + 1:
                nc.sync.dma_start(out=u_rows[:], in_=U.rearrange("(p t) c -> p t c", t=PACK))
        nc.sync.dma_start(out=v_rows[:], in_=V.rearrange("(h p t) r -> p h t r", p=P, t=PACK))
        nc.sync.dma_start(out=a_rows[:], in_=A.rearrange("(p t) c -> p t c", t=PACK))
        nc.sync.dma_start(out=e_bf[:], in_=e.rearrange("(p t) -> p t", t=PACK))
        nc.sync.dma_start(out=g_spread[:], in_=g.partition_broadcast(P))

        planes = {}
        grouped = {}
        batch = {}
        mx = {}

        def plane_tile(key, columns, dtype, tag):
            if key not in planes:
                planes[key] = stage.tile([P, PACK, columns], dtype, name=tag, tag=tag)
            return planes[key]

        def widen(kind, s, t, on_vector=False, half=None):
            scale = scale_first[kind][:, s, t : t + 1] if s < EARLY else scale_rest[kind][:, s - EARLY, t : t + 1]
            if half is None:
                target = plane_tile((kind, s), raw[kind, s].shape[2], BF16, "wide_" + kind)
                source = raw[kind, s][:, t, :].bitcast(FP8)
            else:
                target = plane_tile((kind, s, half), W, BF16, "wide_" + kind)
                source = raw[kind, s][:, t, half * W : (half + 1) * W].bitcast(FP8)
            if on_vector:
                nc.vector.tensor_scalar(out=target[:, t, :], in0=source, scalar1=scale, scalar2=None, op0=MULT)
            else:
                nc.scalar.activation(out=target[:, t, :], in_=source, func=COPY, scale=scale)

        def new_batch(key, names, slots=1, own_tag=None):
            tag = own_tag or "grouped%d" % slots
            tile = stage.tile([P, slots * W * PACK], BF16, name=tag, tag=tag, align_bytes=64, bufs=1 if own_tag else 3)
            batch[key] = (tile, names)
            for n, name in enumerate(names):
                grouped[name] = tile[:, n * W * PACK : (n + 1) * W * PACK]

        def interleave_vector(target, source):
            nc.vector.tensor_copy(
                out=target.rearrange("p (c i t) -> p c t i", i=4, t=PACK),
                in_=source.rearrange("p t (c i) -> p c t i", i=4),
            )

        def interleave_f(s):
            nc.vector.tensor_copy(
                out=grouped["f%d" % s].rearrange("p (j n i t) -> p n t i j", j=PACK, i=2, t=PACK),
                in_=planes["f", s][:].rearrange("p t (n i j) -> p n t i j", i=2, j=PACK),
            )

        def interleave_scalar(target, source):
            nc.scalar.copy(out=target.rearrange("p (c t) -> p c t", t=PACK), in_=source.rearrange("p t c -> p c t"))

        def column_half(name, source, n):
            return grouped[name][:, n * 2 * W : (n + 1) * 2 * W], source[:, :, n * W // 2 : (n + 1) * W // 2]

        woven = {}

        def weave(source, banks):
            columns = source.rearrange("p t c -> p c t")
            for n in range(2):
                woven[n] = bank(banks[n], [P, 2, W], "woven", BF16)
                for q in range(2):
                    first = (2 * n + q) * P
                    nc.tensor.matmul(woven[n][:, q, :], lhsT=ident_bf[:], rhs=columns[:, first : first + P, :], start=True, stop=True)

        def weave_out(name, n):
            nc.scalar.copy(out=grouped[name][:, n * 2 * W : (n + 1) * 2 * W], in_=woven[n][:].rearrange("p q c -> p (q c)"))

        def quantize(key, cols=None, rotating=False):
            tile, names = batch[key]
            columns = len(names) * W
            if key not in mx:
                pool, suffix = (stage, "rotating") if rotating else (keep, key)
                codes = pool.tile([P, columns], U32, name="codes_" + suffix, align_bytes=64)
                scales = pool.tile([P, columns], U8, name="scales_" + suffix, align_bytes=64)
                mx[key] = (codes, scales)
                for n, name in enumerate(names):
                    mx[name] = (codes[:, n * W : (n + 1) * W], scales[:, n * W : (n + 1) * W])
            codes, scales = mx[key]
            lo, hi = cols or (0, columns)
            nc.vector.quantize_mx(out=codes[:, lo:hi].bitcast(FP8X4), scales=scales[:, lo:hi], in_=tile[:, lo * PACK : hi * PACK])

        def mx_pass(out, left, block, right, start, stop):
            cols = slice(block * P, (block + 1) * P)
            nc.tensor.matmul_mx(
                out=out,
                lhsT=mx[left][0][:, cols].bitcast(FP8X4),
                lhsT_scale=mx[left][1][:, cols],
                rhs=mx[right][0].bitcast(FP8X4),
                rhs_scale=mx[right][1],
                start=start,
                stop=stop,
            )

        gram = {}

        def gram_pass(s, half, t):
            if s == 0:
                gram[half, t] = bank(PACK * half + t, [P, W], "gram")
            mx_pass(gram[half, t][:], "f%d" % s, t, "h%d_%d" % (s, half), s == 0, s == LAST)

        turned = {}

        def turn(key, rows, b):
            turned[key] = bank(b, [P, 2, 2, P], "turned")
            for j in range(2):
                words = rows[:, j, :].bitcast(F32)
                for u in range(2):
                    nc.tensor.transpose(turned[key][:, j, u, :], words[:, u::2], ident[:])

        def turn_out(key, target):
            nc.scalar.copy(
                out=target.bitcast(F32).rearrange("p (j r u) -> p j r u", j=2, u=2),
                in_=turned[key][:].rearrange("p j u r -> p j r u"),
            )

        def kept_names(k):
            return ["f%d" % k if k < PASSES else "h%d_1" % LAST] + (["h%d_1" % (k - 2)] if k >= 2 else [])

        new_batch("kept0", kept_names(0), slots=2)
        for k in range(PASSES):
            new_batch("kept%d" % (k + 1), kept_names(k + 1), slots=2, own_tag="grouped_late" if k == LAST else None)
            if k < LAST:
                for t in range(H_PLANES_ON_VECTOR if k == 0 else 0, PACK):
                    widen("h", k, t)
                    if 1 <= k <= WOVEN and t >= 2:
                        weave_out("h%d_1" % (k - 1), t - 2)
            else:
                for half in range(HALVES):
                    for t in range(PACK):
                        widen("h", k, t, half=half)
            if k == U_PERIOD + 1:
                new_batch("u_batch", ["u"], own_tag="grouped_weights")
                for pair in range(2):
                    turn_out(("u", pair), grouped["u"][:, pair * 2 * W : (pair + 1) * 2 * W])
            if k == 0:
                for t in range(PACK):
                    widen("f", 0, t, on_vector=True)
                for t in range(H_PLANES_ON_VECTOR):
                    widen("h", 0, t, on_vector=True)
            if k < WOVEN:
                weave(planes["h", k][:, :, W:C2], WEAVE_BANKS)
            if k == U_PERIOD:
                for pair in range(2):
                    turn(("u", pair), u_rows[:, 2 * pair : 2 * pair + 2, :], U_BANKS[pair])
            if k == LAST:
                for t in range(2, PACK):
                    for s in range(k - 2):
                        gram_pass(s, 1, t)
            interleave_f(k)
            if k >= 1:
                new_batch("first%d" % (k - 1), ["h%d_0" % (k - 1)])
                interleave_vector(grouped["h%d_0" % (k - 1)], planes["h", k - 1][:, :, 0:W])
                if k > WOVEN:
                    interleave_vector(grouped["h%d_1" % (k - 1)], planes["h", k - 1][:, :, W:C2])
            if k < LAST:
                for t in range(PACK):
                    widen("f", k + 1, t, on_vector=True)
            if k == U_PERIOD + 2:
                quantize("u_batch")
            quantize("kept%d" % k)
            if k >= 1:
                quantize("first%d" % (k - 1), rotating=True)
                for t in range(PACK):
                    gram_pass(k - 1, 0, t)
            if 2 <= k < LAST:
                for t in range(2):
                    gram_pass(k - 2, 1, t)
            if k + BYTE_BUFS < PASSES:
                load_pass(k + BYTE_BUFS, whole)

        free_banks = []
        held = {}

        def take(key):
            held[key] = free_banks.pop(0)
            return held[key]

        def release(key):
            free_banks.append(held[key])

        def make_d(half, t):
            d = plane_tile(("d", half), W, F32, "wide_h")
            nc.vector.scalar_tensor_tensor(
                out=d[:, t, :], in0=gram[half, t][:], scalar=1.0 / PIXELS,
                in1=a_rows[:, t, half * W : (half + 1) * W], op0=MULT, op1=SUBTRACT,
            )
            free_banks.append(PACK * half + t)

        def make_de(half, t):
            de = plane_tile(("de", half), W, BF16, "wide_f")
            nc.scalar.activation(out=de[:, t, :], in_=planes["d", half][:, t, :], func=COPY, scale=e_col[:, t : t + 1])

        dg = {}

        def make_dg(half, pair):
            dg[half, pair] = stage.tile([P, 2, W], BF16, name="dg", bufs=HALVES * 2)
            gains = g_spread[:, half * W : (half + 1) * W].unsqueeze(1).to_broadcast([P, 2, W])
            nc.vector.tensor_tensor(out=dg[half, pair][:], in0=planes["d", half][:, 2 * pair : 2 * pair + 2, :], in1=gains, op=MULT)

        def turn_dg(half, pair):
            turn(("dg", half, pair), dg[half, pair], take(("dg", half, pair)))

        def turn_dg_out(half, pair):
            turn_out(("dg", half, pair), grouped["dg%d" % pair][:, half * 2 * W : (half + 1) * 2 * W])
            release(("dg", half, pair))

        def quantize_dg(half, pair):
            lo = pair * W + half * 2 * P
            quantize("dg_batch", (lo, lo + 2 * P))

        sums = {}

        def z_pass(half, j):
            sums["z", half, j] = bank(take(("z", half, j)), [P, W], "z_sum")
            mx_pass(sums["z", half, j][:], "u", j, "de%d" % half, True, True)

        def y_pass(t, half):
            if half == 0:
                sums["y", 0, t] = bank(take(("y", 0, t)), [P, R], "y_sum")
            mx_pass(sums["y", 0, t][:], "dg%d" % (t // 2), 2 * half + t % 2, "v%d" % half, half == 0, half == HALVES - 1)

        out_rows = {"y": out_0.rearrange("(p t) r -> p t r", t=PACK), "z": out_1.rearrange("(p t) c -> p t c", t=PACK)}

        def store(which, half, t, on_vector=False):
            result = stage.tile([P, W], F32, name="result", bufs=RESULT_BUFS)
            if on_vector:
                nc.vector.tensor_copy(out=result[:], in_=sums[which, half, t][:])
            else:
                nc.scalar.copy(out=result[:], in_=sums[which, half, t][:])
            nc.sync.dma_start(out=out_rows[which][:, t, half * W : (half + 1) * W], in_=result[:])
            release((which, half, t))

        new_batch("v1_batch", ["v1"], own_tag="grouped_weights")
        new_batch("first_last", ["h%d_0" % LAST])
        new_batch("dg_batch", ["dg0", "dg1"], slots=2)
        interleave_scalar(grouped["h%d_1" % LAST], planes["h", LAST, 1][:])
        for n in range(2):
            interleave_scalar(*column_half("v1", v_rows[:, 1], n))
        interleave_vector(grouped["h%d_0" % LAST], planes["h", LAST, 0][:])
        nc.vector.tensor_copy(out=e_col[:], in_=e_bf[:])
        quantize("first_last", rotating=True)
        quantize("kept%d" % PASSES)

        new_batch("v0_batch", ["v0"], own_tag="grouped_late")
        nc.gpsimd.tensor_scalar(
            out=grouped["v0"].rearrange("p (c t) -> p c t", t=PACK), in0=v_rows[:, 0].rearrange("p t c -> p c t"),
            scalar1=1.0, scalar2=0.0, op0=MULT, op1=ADD,
        )
        for t in range(PACK):
            gram_pass(LAST, 0, t)
        for t in range(PACK):
            for s in range(LAST - 2, PASSES):
                gram_pass(s, 1, t)

        for t in range(PACK):
            make_d(0, t)
            make_de(0, t)
        new_batch("de0_batch", ["de0"])
        weave(planes["de", 0][:], [take(("woven", n)) for n in range(2)])
        for t in range(PACK):
            make_d(1, t)
        for t in range(PACK):
            make_de(1, t)
            if t >= 2:
                weave_out("de0", t - 2)
                release(("woven", t - 2))

        for half in range(HALVES):
            make_dg(half, 0)
            turn_dg(half, 0)
        quantize("de0_batch")
        for j in range(PACK):
            z_pass(0, j)
        new_batch("de1_batch", ["de1"])
        interleave_scalar(*column_half("de1", planes["de", 1][:], 0))
        for half in range(HALVES):
            turn_dg_out(half, 0)
        for j in range(2):
            store("z", 0, j)
        interleave_vector(*column_half("de1", planes["de", 1][:], 1))
        make_dg(0, 1)
        quantize("de1_batch")
        for j in range(2):
            z_pass(1, j)
        for j in range(2, PACK):
            store("z", 0, j)
        for j in range(2, PACK):
            z_pass(1, j)
        quantize_dg(0, 0)
        make_dg(1, 1)
        for half in range(HALVES):
            turn_dg(half, 1)
        for j in range(2):
            store("z", 1, j)
        quantize("v0_batch")
        quantize_dg(1, 0)
        quantize("v1_batch")
        turn_dg_out(0, 1)
        for t in range(2):
            y_pass(t, 0)
        store("z", 1, 2)
        quantize_dg(0, 1)
        for t in range(2):
            y_pass(t, 1)
        turn_dg_out(1, 1)
        store("z", 1, 3, on_vector=True)
        for t in range(2, PACK):
            y_pass(t, 0)
        quantize_dg(1, 1)
        for t in range(2, PACK):
            y_pass(t, 1)
        for t in range(PACK):
            store("y", 0, t, on_vector=t in (1, 2))
